import numpy as np, ml_dtypes
CORES = [66,74,82,90,194,202,210,218]
N = 8
import mx_ref
BF = ml_dtypes.bfloat16
def pick(q, e):
    c = np.concatenate([q[0].reshape(128, -1, 4), np.zeros((128, 1, 4), np.uint8)], axis=1); s = np.concatenate([q[1], np.ones((16, 1), np.uint8)], axis=1)
    return (np.ascontiguousarray(c[:, e].reshape(128, -1)), np.ascontiguousarray(s[:, e]))
def join(*qs):
    return (np.concatenate([q[0] for q in qs], axis=1), np.concatenate([q[1] for q in qs], axis=1))
def put(q, e, v):
    c, s = q[0].reshape(128, -1, 4).copy(), q[1].copy(); c[:, e] = v[0].reshape(128, -1, 4); s[:, e] = v[1]
    return (c.reshape(128, -1), s)
def pk(c, s):
    return (np.ascontiguousarray(c), mx_ref.live(s))
def emit(q):
    return q[0], q[1]
def decode(q):
    o = []
    for b in range(4):
        e = np.zeros((128, 128, 4), np.float32); e[np.arange(128), np.arange(128), b] = 1
        o.append(mx_ref.matmul(mx_ref.quantize(e.reshape(128, 512).astype(BF)), q))
    return np.stack(o, axis=2).reshape(128, -1)
def cut(t, i, w=512):
    return t[:, w * i:w * i + w]
def f(rng, *shape):
    return mx_ref.flush((rng.standard_normal(shape, dtype=np.float32) * np.exp2(rng.integers(-2, 3, shape[:-1] + (1,)))).astype(BF))
def wide(rng, *shape, cols=0):
    v = rng.standard_normal(shape, dtype=np.float32) * np.exp2(rng.integers(-12, 13, shape)).astype(np.float32)
    if cols: v *= np.repeat(np.exp2(rng.integers(-cols, cols + 1, shape[:-2] + (1, shape[-1] // 4))) * (rng.random(shape[:-2] + (1, shape[-1] // 4)) > 0.0625), 4, axis=-1).astype(np.float32)
    return mx_ref.flush(v.astype(BF))
T, L, O, LV, V, F = 24, 8, 2, 3, 168, 24
DI, DJ = np.array([1, 1, 0, 0]), np.array([1, 0, 1, 0])
def align(g):
    n = g.shape[0]
    p, back = np.zeros((n, L, L), np.float32), np.full((n, L, L), 3)
    for i in range(L):
        for j in range(L):
            if i == 0 and j == 0:
                p[:, i, j] = g[:, i, j]
                continue
            if i == 0: best, back[:, i, j] = p[:, i, j - 1], 2
            elif j == 0: best, back[:, i, j] = p[:, i - 1, j], 1
            else:
                c = np.stack([p[:, i - 1, j - 1], p[:, i - 1, j], p[:, i, j - 1]])
                best, back[:, i, j] = np.max(c, axis=0), np.argmax(c, axis=0)
            p[:, i, j] = g[:, i, j] + best
    m, i, j, low = np.arange(n), np.full(n, L - 1), np.full(n, L - 1), np.zeros((n, L), int)
    for s in range(2 * L - 1):
        low[m, i] = j
        k = back[m, i, j]
        i, j = i - DI[k], j - DJ[k]
    return low
def clear(v):
    v = v.astype(np.float32)
    v[np.abs(v) < np.float32(2.0 ** -14)] = 0
    return v.astype(BF)
def lay(v):
    return np.ascontiguousarray(v.transpose(0, 3, 1, 2, 4)).reshape(N, 128, 4 * T * L).astype(np.float32).astype(BF)
def setup_inputs(rng):
    return {"x": clear(f(rng, N, 128, 4 * T * L)), "w": f(rng, N, 128, 512 * O)}
def setup_inputs_ties(rng):
    kind = (np.arange(T) // N) % 3
    u = rng.choice([-1.0, 1.0], (T, 128, 4)) * np.exp2(rng.integers(-3, 4, (T, 1, 1)))
    s = rng.integers(-1, 2, (N, T, L)).astype(np.float64)
    m = rng.choice([-1.0, 1.0], (N, T, L))
    s[:, :, 0] = 1
    m[:, :, 0] = 1
    m[1::2] = 0
    s[:, kind == 0] = 1
    s[:, kind == 1] = m[:, kind == 1]
    return {"x": lay(s[:, :, :, None, None] * u[None, :, None]), "w": f(rng, N, 128, 512 * O)}
def setup_inputs_near(rng):
    kind = (np.arange(T) // N) % 3
    even, one = kind != 1, kind == 1
    u = rng.choice([-1.0, 1.0], (T, 1, 128, 4))
    v = np.zeros((N, T, L, 128, 4))
    v[:, even, :, :120] = u[even][:, :, :120]
    for r in range(N):
        v[r][one, 0, :64] = 4 * u[one][:, 0, :64]
        v[r][one, 1:, 64 + 6 * r:70 + 6 * r] = rng.choice([-1.0, 1.0], (int(np.count_nonzero(one)), L - 1, 6, 4))
    a = rng.integers(1, 4, (N, T, L)) * rng.choice([-1.0, 1.0], (N, T, L))
    a[:, kind == 2] = 1
    a[0::2][:, kind == 2, L - 1] = 3
    a[1::2][:, kind == 2, 0] = 3
    v[:, :, :, 127, 0] = a * np.where(one, 2.0 ** -6, 2.0 ** -5)[None, :, None]
    return {"x": lay(v * np.exp2(rng.integers(-3, 4, (1, T, 1, 1, 1)))), "w": f(rng, N, 128, 512 * O)}
def setup_inputs_far(rng):
    kind = (np.arange(T) // N) % 3
    deep, side = kind == 2, np.arange(T) // 2 % 2 == 1
    v = 1.5 + 0.5 * rng.random((N, T, L, 128, 4))
    v[:, deep] = 1
    ones = np.array([bin(k).count("1") for k in range(N)])
    c = ones[np.arange(N)[:, None] ^ rng.integers(0, N, T)[None, :]]
    e = -rng.integers(3, 9, (N, T, L))
    e[:, :, 0] = 0
    low = np.exp2(29.0 - c[:, :, None] + e) * (1 - 2 * (c % 2))[:, :, None]
    mixed = np.exp2(rng.integers(20, 30, (N, T, L))) * rng.choice([-1.0, 1.0], (N, T, L))
    mixed[:, :, 0] = 2.0 ** 29
    s = np.where((kind == 0)[None, :, None], low, mixed)
    s[0::2][:, deep] = 2.0 ** 30
    s[1::2][:, deep] = -2.0 ** 30
    s[0::2][:, deep & ~side, L - 1] = 2.0 ** 20
    s[1::2][:, deep & side, L - 1] = -2.0 ** 20
    return {"x": lay(v * s[:, :, :, None, None]), "w": f(rng, N, 128, 512 * O)}
def setup_inputs_warp(rng):
    p = rng.standard_normal((T, L, 128, 4)) * np.exp2(rng.integers(-2, 3, (T, 1, 128, 1)))
    i = np.sort(rng.integers(0, L, (N, T, L)), axis=2)
    v = p[np.arange(T)[None, :, None], i] + 0.25 * rng.standard_normal((N, T, L, 128, 4))
    return {"x": clear(lay(v)), "w": f(rng, N, 128, 512 * O)}
def setup_inputs_spread(rng):
    return {"x": clear(wide(rng, N, 128, 4 * T * L, cols=6)), "w": f(rng, N, 128, 512 * O)}
def check_inputs(d):
    b = []
    for k, least in (("x", 2.0 ** -14), ("w", 2.0 ** -30)):
        v = np.abs(d[k].astype(np.float32))
        if not (np.isfinite(v).all() and ((v == 0) | (v >= least) & (v <= 2.0 ** 30)).all()): b.append("a value of " + k)
    return b
def reference(x, w):
    y, pt = np.zeros((N, 128, O * V), np.float32), np.zeros((N, 1, V), np.float32)
    oc, osc = np.zeros((N, 128, 4 * F), np.uint8), np.zeros((N, 16, F), np.uint8)
    wq = [[mx_ref.quantize(np.ascontiguousarray(cut(w[r], o))) for o in range(O)] for r in range(N)]
    held = [mx_ref.quantize(np.ascontiguousarray(x[r])) for r in range(N)]
    at = 0
    for b in range(LV):
        n = T >> (b + 1)
        h = n * L
        new = []
        for r in range(N):
            p = r ^ (1 << b)
            k = np.arange((r >> b) & 1, T >> b, 2)
            e = (k[:, None] * L + np.arange(L)).reshape(-1)
            lower, upper = pick(held[min(r, p)], e), pick(held[max(r, p)], e)
            g = mx_ref.matmul(pick(lower, np.concatenate([np.arange(h), np.full(128 - h, -1)])), upper)[:h].reshape(n, L, n, L)
            j = align(g[np.arange(n), :, np.arange(n), :])
            met = pick(upper, (np.arange(n)[:, None] * L + j).reshape(-1))
            v = decode(join(lower, met))
            m = mx_ref.quantize(np.ascontiguousarray(((v[:, :4 * h] + v[:, 4 * h:]) * np.float32(0.5)).astype(BF)))
            pt[r, 0, at:at + h] = j.reshape(-1)
            for o in range(O): y[r, :, o * V + at:o * V + at + h] = mx_ref.matmul(wq[r][o], m)
            new.append(m)
        held = new
        at += h
    for r in range(N): oc[r], osc[r] = emit(held[r])
    return {"y": y, "pt": pt, "oc": oc, "osc": osc}

@@ -1,0 +1,388 @@
+from concourse.bass import DstId, RemoteDMATransfer
+from concourse.mybir import dt, AluOpType, ActivationFunctionType
+
+SCRATCH = {"ps": ("psum", [128, 4096], "float32")}
+for _n, _w in dict(x=192, w=256, g=128, o=144, l0=256, l1=320, m0=256, m1=128, m2=128, e=512, u=128, d=128).items():
+    SCRATCH["q" + _n] = ("sbuf", [128, _w], "float8_e4m3fn_x4")
+    SCRATCH["s" + _n] = ("sbuf", [128, _w], "uint8")
+for _d, _b in {"bfloat16": dict(xt=[768], wt=[1024], et=[516], ut=[512], ones=[128], ident=[128], u64=[64], dg=[816], mt=[1056],
+                                d0=[1024], d1=[800], d2=[352], am0=[512], am1=[448], am2=[96]),
+               "int32": dict(pi=[1], pj=[8], fa=[136], fb=[136]), "uint16": dict(ls=[128], off=[96]),
+               "float32": dict(pf=[8], rt=[16], ct=[128], i4=[4], m4=[12], key=[304], wd=[304], pwn=[96], pwb=[64], tt=[8, 32], gs=[8, 32],
+                               z=[16, 36], cs=[8, 16], cd=[16, 16], wr=[8, 8], ptf=[24], yt=[512], yo=[336])}.items():
+    for _n, _w in _b.items():
+        SCRATCH[_n] = ("sbuf", [128] + _w, _d)
+SEMAPHORES = ["v", "s", "p", "g", "ldx", "ldw", "a1", "a2", "loc", "o1", "o2"]
+A = AluOpType
+COPY = ActivationFunctionType.Copy
+LOW = -1e29
+BG, BR, BY, BD = 0, 512, 1024, 2048
+ORDER = ("s0 m1 s1 m2 c1-3 s2 p1-2 m3 x1 s3 k1 m4 x2 c4-7 s4 k2 p3-4 m5 x3 s5 k3 m6 x4 c8-11 s6 k4 p5-6 m7 x5 s7 k5 "
+         "c12-14 x6 p7 k6 x7 k7").split()
+
+
+def fit(vals, dims):
+    steps, stride = [], len(vals)
+    for n in dims:
+        stride //= n
+        steps.append(vals[stride] - vals[0] if n > 1 else 0)
+    for k in range(len(vals)):
+        rest, tot = k, vals[0]
+        for n, st in zip(reversed(dims), reversed(steps)):
+            tot += (rest % n) * st
+            rest //= n
+        assert tot == vals[k]
+    return [[st, n] for st, n in zip(steps, dims)], vals[0]
+
+
+def piece(kind, dims, f):
+    idx = [[]]
+    for n in dims:
+        idx = [a + [k] for a in idx for k in range(n)]
+    rows = [f(*a) for a in idx]
+    return {"kind": kind, "dims": dims, "key": [t[0] for t in rows], "base": [t[1] for t in rows], "src": [t[2] for t in rows]}
+
+
+def rank_program(g, core, T, topo):
+    r = T.rank_of(core)
+    if r is None:
+        return
+    b0, b1, b2 = r & 1, (r >> 1) & 1, (r >> 2) & 1
+    V, S, P = g.vector, g.scalar, g.tensor
+    queue = {"v": V, "s": S, "p": P, "g": g, "y": g.sync}
+    count = {k: 0 for k in SEMAPHORES}
+    seen = {}
+
+    def wait(q, deps):
+        need = {}
+        for d in deps:
+            if d is not None:
+                need[d[0]] = max(need.get(d[0], 0), d[1])
+        for s, n in need.items():
+            if seen.get((q, s), 0) < n:
+                queue[q].wait_ge(T.sem[s], n)
+                seen[(q, s)] = n
+
+    def op(q, deps, f):
+        wait(q, deps)
+        f().then_inc(T.sem[q], 1)
+        count[q] += 1
+        return (q, count[q])
+
+    def dma(q, sem, deps, out, in_):
+        wait(q, deps)
+        queue[q].dma_start(out, in_).then_inc(T.sem[sem], 16)
+        count[sem] += 16
+        return (sem, count[sem])
+
+    def iota(out, vals, dims, deps=()):
+        pat, base = fit(vals, dims)
+        return op("g", deps, lambda: g.iota(out, pat, base, 0, allow_small_or_imprecise_dtypes=True))
+
+    def mset(ap, c, deps=()):
+        return op("v", deps, lambda: V.memset(ap, c))
+
+    def ts(out, in0, s1, o0, s2=None, o1=None, deps=()):
+        if s2 is None:
+            return op("v", deps, lambda: V.tensor_scalar(out, in0, s1, None, o0))
+        return op("v", deps, lambda: V.tensor_scalar(out, in0, s1, s2, o0, o1))
+
+    def tt(out, in0, in1, o, deps=()):
+        return op("v", deps, lambda: V.tensor_tensor(out, in0, in1, o))
+
+    def cp(out, in_, deps=()):
+        return op("v", deps, lambda: V.tensor_copy(out, in_))
+
+    def scan(out, d0, d1, first, o0, o1, deps):
+        return op("v", deps, lambda: V.tensor_tensor_scan(out, d0, d1, first, o0, o1))
+
+    def act(out, in_, scale=1.0, deps=()):
+        return op("s", deps, lambda: S.activation(out, in_, COPY, scale=scale))
+
+    def gat(out, in_, deps):
+        return op("s", deps, lambda: S.activation(out, in_, COPY))
+
+    def quant(n_, a, n, src, deps):
+        return op("v", deps, lambda: V.quantize_mx(T["q" + n_][:, a:a + n], T["s" + n_][:, a:a + n], src))
+
+    def mm(bank, st, mv, start, stop, deps):
+        (s, sa), (m, ma, n) = st, mv
+        return op("p", deps, lambda: P.matmul_mx(T.ps[:, bank:bank + n], T["q" + s][:, sa:sa + 128], T["s" + s][:, sa:sa + 128],
+                                                 T["q" + m][:, ma:ma + n], T["s" + m][:, ma:ma + n], start, stop))
+
+    def at0(x, lo, a, i):
+        u = (x ^ b1) + 2 * (lo ^ b2)
+        return (36 * a + u, 8 * u + 32 * a, 128 + 16 * i + u + 4 * a)
+    if b1 == 0:
+        pc0 = [piece("blk", [8, 2, 4], lambda i, lo, a, x=x: at0(x, lo, a, i)) for x in (0, 1)]
+        cB1, cB2, cA1, cA2 = 88, 0, 136, 24
+    else:
+        pc0 = [piece("nat", [2, 3, 8], lambda lo, a, i, x=x: at0(x, lo, a, i)) for x in (1, 0)]
+        cB1, cB2, cA1, cA2 = 0, 48, 72, 136
+
+    def own1(lo, m, i):
+        return (36 * lo + m, cB1 + 24 * lo + 8 * m, cA1 + 8 * i + 4 * lo + m)
+
+    def far1(m, i):
+        return (68 + m, cB2 + 8 * m, cA2 + 8 * i + 4 + m)
+    if b2 == 0:
+        pc1 = [piece("blk", [8, 2, 4], lambda i, lo, m: own1(lo, m, i)), piece("nat", [3, 8], far1)]
+    else:
+        pc1 = [piece("blk", [8, 2, 4], lambda i, h, m: far1(m, i)), piece("nat", [2, 3, 8], own1)]
+    pcs = [pc0, pc1, [piece("nat", [3, 8], lambda m, i: (64 + m, 64 + 8 * m, 8 * i + m))]]
+    ncol = [sum(len(p["key"]) for p in pc) for pc in pcs]
+    WO = [0, 144, 272]
+    MO = [544, 96, 0]
+    LG, LO, LA, LY = 0, 8, [18, 50, 78], [84, 90]
+    OO = [0, 32, 64]
+
+    hx = dma("y", "ldx", [], T.xt[:], T.x[:])
+    hw = dma("y", "ldw", [], T.wt[:], T.w[:])
+
+    hones = mset(T.ones[:], 1.0)
+    hp = op("g", [], lambda: g.iota(T.pi[:], [[0, 1]], 0, 1))
+    if b0 == 0:
+        iota(T.ct[:, LG:LG + 8], [8 + i for i in range(8)], [8])
+        hct = iota(T.ct[:, LO:LO + 9], [i for i in range(9)], [9])
+        nG, nO = 128, 144
+    else:
+        iota(T.ct[:, LG:LG + 8], [32 * c for c in range(8)], [8])
+        hct = iota(T.ct[:, LO:LO + 8], [8 + 32 * c for c in range(8)], [8])
+        nG, nO = 96, 128
+    hid = op("g", [hones], lambda: g.affine_select(T.ident[:], T.ones[:], [[-1, 128]], A.is_equal, 0.0, 0, 1))
+    hu64 = op("g", [hones], lambda: g.affine_select(T.u64[:], T.ones[:, 0:64], [[1, 4], [0, 4], [-1, 4]], A.is_equal, 0.0, 0, 0))
+    hi4 = iota(T.i4[:], [0, 1, 2, 3], [4])
+    for k, (sh, mk) in enumerate([(0, 15), (0, 7), (3, 1), (2, 3), (0, 3), (0, 127)]):
+        hj = ts(T.pj[:, k:k + 1], T.pi[:], sh, A.logical_shift_right, mk, A.bitwise_and, deps=[hp])
+    hdg = mset(T.dg[:], 0.0)
+    hpf = cp(T.pf[:, 0:6], T.pj[:, 0:6], [hj])
+    p16, p8, ph, p4, pq, pp = [T.pf[:, k:k + 1] for k in range(6)]
+    mset(T.cs[:, 0, 0:1], 4.0)
+    if b0 == 0:
+        h = ts(T.rt[:, 0:1], p16, 11.0, A.min, 16.0, A.mult, deps=[hpf])
+    else:
+        h = ts(T.rt[:, 0:1], ph, 16.0, A.mult, p8, A.add, deps=[hpf])
+    mset(T.cs[:, 0, 1:16:2], 1.0 - 2.0 ** -22)
+    hl = ts(T.ls[:, 0:LO + nO // 16], T.ct[:, 0:LO + nO // 16], T.rt[:, 0:1], A.add, 191.0, A.min, deps=[h, hct])
+    hz = quant("l0", 96 if b0 == 0 else 128, 128, T.dg[:, 304:816], [hdg])
+
+    for i in range(8):
+        hpw = act(T.pwn[:, i:96:8], T.ones[:, 0:12], 8.0 ** (8 - i) if i else 0.0, deps=[hones])
+    for e in range(4):
+        act(T.et[:, e:512:4], T.ident[:], 1.0 if e == 3 else 0.0, deps=[hid])
+    he = act(T.et[:, 512:516], T.ones[:, 0:4], 0.0)
+    for i in range(1, 8):
+        act(T.cd[:, 2 * i, 1:16:2], T.ones[:, 0:8], -sum(8.0 ** (k - 8) for k in range(1, i + 1)))
+
+    hqx = quant("x", 0, 192, T.xt[:], [hx])
+
+    def pick(b, n, lst):
+        o = T.ls[:, lst:lst + n // 16]
+        hc = cp(T["q" + b][:, 0:n].bitcast(dt.uint32), T.qx[:, 0:192].bitcast(dt.uint32).indirect(o), [hqx, hl])
+        return hc, gat(T["s" + b][:, 0:n], T.sx[:, 0:192].indirect(o), [hqx, hl])
+    hgc, hgs = pick("g", nG, LG)
+
+    def bits(es):
+        return sum(1 << e for e in es)
+    mate = T.cores[r ^ 1]
+    rid, pid = topo.addr(mate, core)
+    es = topo.engines(core, mate)
+    half = len(es) // 2
+    wait("g", [hgc])
+    g.remote_dma(T.ql0[:, 0:nG].bitcast(dt.uint8), T.qg[:, 0:nG].bitcast(dt.uint8), T.sem.a1, T.sem.loc, pid, rid, bits(es[:half]))
+    wait("g", [hgs])
+    g.remote_dma(T.sl0[:, 0:nG], T.sg[:, 0:nG], T.sem.a1, T.sem.loc, pid, rid, bits(es[half:]))
+    count["loc"] += 2 * half
+    ha1 = ("a1", len(topo.engines(mate, core)) // 2 * 2)
+
+    hoc, hos = pick("o", nO, LO)
+    for b in range(4):
+        hqe = quant("e", 128 * b, 128, T.et[:, 3 - b:515 - b], [he])
+    mset(T.z[:], LOW)
+    for i in range(8):
+        hpb = act(T.pwb[:, 8 * i:8 * i + 8], T.ones[:, 0:8], 8.0 ** (8 - i) if i else 0.0)
+    hkey = []
+    for L in range(3):
+        v, c = WO[L], LA[L]
+        for p in pcs[L]:
+            n = len(p["key"])
+            iota(T.key[:, v:v + n], p["key"], p["dims"], deps=[("g", count["g"])] if (L, v) == (1, WO[1]) else [])
+            hk = iota(T.ct[:, c:c + n // 4], [4 * s for s in p["src"][0::4]], p["dims"][:-1] + ([2] if p["dims"][-1] == 8 else []))
+            v += n
+            c += n // 4
+        hkey.append(hk)
+        if L == 0:
+            for L2 in range(3):
+                v = WO[L2]
+                for p in pcs[L2]:
+                    hb = iota(T.dg[96:97, v:v + len(p["key"])], p["base"], p["dims"], deps=[hdg, hk])
+                    v += len(p["key"])
+    iota(T.ct[:, LY[0]:LY[0] + 6], [(4 * (c ^ b2) + a) if b1 == 0 else (24 * (c ^ b2) + 8 * a) for a in range(3) for c in range(2)], [3, 2])
+    hcy = iota(T.ct[:, LY[1]:LY[1] + 3], [m if b2 == 0 else 88 + 8 * m for m in range(3)], [3])
+
+    free = {"d": None, "y": None}
+
+    def decode_mm(mv, deps):
+        return [mm(BD + 512 * b, ("e", 128 * b), mv, True, True, [hqe, free["d"]] + deps) for b in range(4)]
+
+    def decode_cp(hs, dst, runs):
+        for b in range(4):
+            for (a, n, at) in runs:
+                h = act(T[dst][:, 4 * at + b:4 * (at + n):4], T.ps[:, BD + 512 * b + a:BD + 512 * b + a + n], 0.5, deps=[hs[b]])
+        free["d"] = h
+        return h
+    decode_cp(decode_mm(("o", 0, 128), [hoc, hos]), "d0", [(0, 128, 128 if b0 == 0 else 0)])
+    h = act(T.ut[:, 0:64], T.u64[:], 4.0, deps=[hu64])
+    for i in range(1, 8):
+        hcd = act(T.wr[:, i, :], T.ones[:, 0:8], 1.0 + 8.0 ** (i - 8))
+        if i in (2, 4, 6):
+            n = 32 << (i // 2)
+            h = act(T.ut[:, n:2 * n], T.ut[:, 0:n], deps=[h])
+    hut = h
+    rts = {}
+
+    def tables(L, quads):
+        for a, c in quads:
+            ts(T.m4[32 * a:32 * a + 32, 4 * L:4 * L + 4], T.i4[32 * a:32 * a + 32, :], float(c), A.add, T.pf[32 * a:32 * a + 32, 5:6], A.is_equal, deps=[hi4, hpf])
+        gams = [4 * (p["src"][1] - p["src"][0]) for p in pcs[L]]
+        for gam in gams:
+            if gam not in rts:
+                k = 1 + len(rts)
+                rts[gam] = (T.rt[:, k:k + 1], ts(T.rt[:, k:k + 1], p4, float(gam), A.mult, pq, A.add, deps=[hpf]))
+        v, n = WO[L], ncol[L]
+        cp(T.wd[:, v + n:v + n + 8], T.pwn[:, 0:8], [hpw])
+        heq = ts(T.key[:, v:v + n], T.key[:, v:v + n], pp, A.is_equal, deps=[hkey[L]])
+        c = LA[L]
+        for p, gam in zip(pcs[L], gams):
+            m = len(p["key"]) // 4
+            hla = ts(T.ls[:, c:c + m], T.ct[:, c:c + m], rts[gam][0], A.add, deps=[rts[gam][1], hkey[L]])
+            c += m
+        for p in pcs[L]:
+            m = len(p["key"])
+            hwd = tt(T.wd[:, v:v + m], T.key[:, v:v + m], T.pwb[:, 0:m] if p["kind"] == "blk" else T.pwn[:, 0:m], A.mult, deps=[heq, hpw, hpb])
+            v += m
+        return hla, hwd
+    if b1 == 1:
+        mset(T.mt[:, 928:1056], 0.0)
+        quant("m0", 128, 128, T.dg[:, 304:816], [hdg])
+    tab = [tables(0, [(0, 0), (1, 36), (2, 72)]), None, None]
+    hqu = quant("u", 0, 128, T.ut[:], [hut])
+
+    def level(L, lo, hi, prods, deps, dec, runs, dcols, mid=None):
+        n, v = ncol[L], WO[L]
+        hla, hwd = tab[L]
+        dw, am = T["d%d" % L][:, 0:4 * dcols], T["am%d" % L][:, 0:4 * n]
+        for k, (st, mv) in enumerate(prods):
+            hg = mm(BG, st, mv, k == 0, k == len(prods) - 1, deps)
+        hs = decode_mm(dec, deps)
+        nt = 2 if L == 0 else 4
+        for k in range(nt):
+            ht = op("v", [hg], lambda: V.transpose(T.tt[lo:hi, 8 // nt * k:8 // nt * (k + 1), :], T.ps[lo:hi, BG + 32 // nt * k:BG + 32 // nt * k + 256 // nt]))
+        at = [8 // nt * (i % nt) + i // nt for i in range(8)]
+        for s in (2, 3):
+            hb2 = act(T.gs[lo:hi, :, s:32:4], T.tt[lo:hi, :, 8 * s:8 * s + 8], T.m4[lo:hi, 4 * L + s:4 * L + s + 1], deps=[ht])
+        for s in (0, 1):
+            h = ts(T.gs[lo:hi, :, s:32:4], T.tt[lo:hi, :, 8 * s:8 * s + 8], T.m4[lo:hi, 4 * L + s:4 * L + s + 1], A.mult, deps=[ht])
+        hd = decode_cp(hs, "d%d" % L, runs)
+        ham = gat(am, dw.indirect(T.ls[:, LA[L]:LA[L] + n // 4]), [hd, hla])
+        if mid is not None:
+            mid()
+        z, cs, cd = T.z, T.cs, T.cd
+        done = {}
+        for tok in ORDER:
+            k, i, j = tok[0], int(tok[1:].split("-")[0]), int(tok[1:].split("-")[-1])
+            if k == "s":
+                done[2 * i] = scan(z[lo:hi, 2 * i, 4:36], z[lo:hi, (2 * i - 1) % 16, 3:35], T.gs[lo:hi, at[i], :], LOW if i else 0.0,
+                                   A.max, A.add, [done[2 * i - 1]] if i else [h, hb2])
+            elif k == "m":
+                done[2 * i - 1] = tt(z[lo:hi, 2 * i - 1, 3:32:4], z[lo:hi, 2 * i - 2, 3:32:4], z[lo:hi, 2 * i - 2, 7:36:4], A.max, deps=[done[2 * i - 2]])
+            elif k == "c":
+                hc = tt(cd[lo:hi, i:j + 1, 0:16:2], z[lo:hi, i:j + 1, 3:32:4], z[lo:hi, i - 1:j, 3:32:4], A.is_le, deps=[done[j]])
+                for row in range(i, j + 1):
+                    done["c", row] = hc
+            elif k == "p":
+                hc = tt(cd[lo:hi, 2 * i - 1:2 * j:2, 1:16:2], T.wr[lo:hi, i:j + 1, :], cd[lo:hi, 2 * i - 1:2 * j:2, 0:16:2], A.subtract, deps=[done["c", 2 * j - 1], hcd])
+                for row in range(i, j + 1):
+                    done["p", row] = hc
+            elif k == "x":
+                done["x", i] = tt(cs[lo:hi, i - 1, 2:16:2], cs[lo:hi, i - 1, 1:14:2], cd[lo:hi, 2 * i - 1, 3:16:2], A.add, deps=[done["p", i], done.get(("k", i - 1))])
+            else:
+                done["k", i] = scan(cs[lo:hi, i, :], cd[lo:hi, 2 * i, :], cs[lo:hi, i - 1, :], 4.0, A.add, A.min, [done["x", i], done["c", 2 * i]])
+        h = ts(T.fa[lo:hi, 0:n + 8], T.wd[lo:hi, v:v + n + 8], cs[lo:hi, 7, 15:16], A.mult, -0.5, A.add, deps=[done["k", 7], hwd])
+        h = ts(T.fb[lo:hi, 0:n + 8], T.fa[lo:hi, 0:n + 8], 7, A.bitwise_and, deps=[h])
+        hdig = cp(T.dg[lo:hi, v:v + n + 8], T.fb[lo:hi, 0:n + 8], [h])
+        h = quant("d", 0, 128, T.dg[:, v:v + 512], [hdig, hb])
+        hpt = act(T.ptf[lo:hi, 8 * L:8 * L + 8], T.dg[lo:hi, v + n:v + n + 8], deps=[hdig])
+        h = mm(BR, ("u", 0), ("d", 0, 128), True, True, [h, hqu])
+        o = T.off[:, OO[L]:OO[L] + n // 4]
+        h = ts(o, T.ps[:, BR:BR + n // 4], pq, A.add, deps=[h])
+        h = tt(T.mt[:, MO[L]:MO[L] + 4 * n], dw.indirect(o), am, A.add, deps=[h, ham])
+        return quant("m%d" % L, 0, 128, T.mt[:, MO[L]:MO[L] + 512], [h]), hpt
+
+    def outputs(L, hm, hqw, hly, at, n):
+        hy = [mm(BY + 512 * o, ("w", 128 * o), ("m%d" % L, 0, 128), True, True, [hm, hqw, free["y"]]) for o in range(2)]
+        hc = [act(T.yt[:, 256 * L + 128 * o:256 * L + 128 * o + 128], T.ps[:, BY + 512 * o:BY + 512 * o + 128], deps=[hy[o]]) for o in range(2)]
+        free["y"] = hc[1]
+        for o in range(2):
+            w0, y0 = 256 * L + 128 * o, 168 * o + at
+            h = gat(T.yo[:, y0:y0 + n], T.yt[:, w0:w0 + 128].indirect(T.ls[:, LY[L]:LY[L] + n // 16]), [hc[o], hly])
+            dma("y", "o1", [h], T.y[:, y0:y0 + n], T.yo[:, y0:y0 + n])
+
+    prods = [(("l0", 0), ("o", 0, 144))] if b0 == 0 else [(("o", 0), ("l0", 0, 144))]
+    hm0, hpt = level(0, 0, 96, prods, [ha1, hz, hoc, hos], ("l0", 0, 128), [(0, 128, 128 * b0)], 256)
+
+    plan = [(2, 64, 0), (6, 64, 64), (4, 0, 0)] if b1 == 0 else [(2, 0, 64), (6, 24, 256), (4, 72, 256)]
+    es = [e for e in topo.engines(core, T.cores[r ^ 2]) if all(e in topo.engines(core, T.cores[r ^ x]) for x in (4, 6))]
+    k4 = len(es) // 4
+    sets = [[es[0:k4], es[k4:2 * k4], es[2 * k4:4 * k4]], [es[2 * k4:3 * k4], es[3 * k4:4 * k4], es[0:2 * k4]]]
+    wait("g", [hm0])
+    for kind in range(2):
+        trs = []
+        for (x, a, at), e in zip(plan, sets[kind]):
+            rid, pid = topo.addr(T.cores[r ^ x], core)
+            if kind == 0:
+                src, dst = T.qm0[:, a:a + 64].bitcast(dt.uint8), T.ql1[:, at:at + 64].bitcast(dt.uint8)
+            else:
+                src, dst = T.sm0[:, a:a + 64], T.sl1[:, at:at + 64]
+            trs.append(RemoteDMATransfer(dst_ids=[DstId(rid=rid, pnc=pid)], dma_engine_mask=bits(e), remote_sem=T.sem.a2, src=src, dst=dst))
+        g.remote_dma_fused(trs, local_sem=T.sem.loc)
+    count["loc"] += 8 * k4
+    ha2 = ("a2", 8 * k4)
+    for a in range(3):
+        dma("y", "o1", [hpt], T.pt[0:1, 32 * a:32 * a + 32], T.ptf[36 * a:36 * a + 4, 0:8])
+
+    decode_cp(decode_mm(("m0", 0, 128), [hm0]), "d1", [(0, 64, cA1)] if b1 == 0 else [(48, 48, cB1)])
+    hqw = quant("w", 0, 256, T.wt[:], [hw])
+    hz1 = quant("l1", 128, 128, T.dg[:, 304:816], [hdg])
+    hp8 = ts(T.rt[:, 12:13], p8, 8.0, A.mult, deps=[hpf])
+    if b2 == 0:
+        mset(T.mt[:, 448:544], 0.0)
+    h0 = ts(T.rt[:, 13:14], ph, 64.0 if b1 == 0 else 48.0, A.mult, T.rt[:, 12:13] if b1 == 0 else p8, A.add, deps=[hp8])
+    h1 = ts(T.rt[:, 14:15], ph, 4.0 if b2 == 0 else -24.0, A.mult, T.rt[:, 12:13] if b2 == 0 else p8, A.add, deps=[hp8])
+    ts(T.ls[:, LY[0]:LY[0] + 6], T.ct[:, LY[0]:LY[0] + 6], T.rt[:, 13:14], A.add, deps=[h0, hcy])
+    hly = ts(T.ls[:, LY[1]:LY[1] + 3], T.ct[:, LY[1]:LY[1] + 3], T.rt[:, 14:15], A.add, deps=[h1, hcy])
+    outputs(0, hm0, hqw, hly, 0, 96)
+    tab[1] = tables(1, [(0, -1), (1, 36), (2, 67)])
+    tab[2] = tables(2, [(2, 64)])
+
+    if b1 == 0:
+        prods, runs = [(("l1", 56), ("m0", 0, 128)), (("l1", 184), ("l1", 0, 128))], [(256, 24, cB2), (0, 112, cA2)]
+    else:
+        prods, runs = [(("m0", 40), ("l1", 0, 128)), (("l1", 184), ("l1", 64, 128))], [(256, 24, cB2), (0, 128, cA1)]
+    hm1, hpt = level(1, 0, 96, prods, [ha2, hz1, hm0], ("l1", 0, 280), runs, 200)
+    for lo in range(2):
+        for m in range(3):
+            k = (lo ^ b2) + 2 * m
+            dma("y", "o1", [hpt], T.pt[0:1, 96 + 8 * k:104 + 8 * k], T.ptf[36 * lo + m:36 * lo + m + 1, 8:16])
+
+    hm2, hpt = level(2, 64, 96, [(("m1", 0), ("m1", 0, 128))], [hm1], ("m1", 0, 128), [(0, 88, 0)], 88,
+                     lambda: outputs(1, hm1, hqw, hly, 96, 48))
+    dma("y", "o1", [hpt], T.pt[0:1, 144:168], T.ptf[64:67, 16:24])
+    dma("y", "o1", [hm2], T.oc[:, 0:96], T.qm2[:, 0:24].bitcast(dt.uint8))
+    for k in range(4):
+        dma("y" if k < 1 else "s", "o1" if k < 1 else "o2", [hm2], T.osc[4 * k:4 * k + 4, 0:24], T.sm2[32 * k:32 * k + 4, 0:24])
+    for o in range(2):
+        h = mm(BY + 512 * o, ("w", 128 * o), ("m2", 0, 128), True, True, [hm2, free["y"]])
+        h = cp(T.yo[:, 168 * o + 144:168 * o + 168], T.ps[:, BY + 512 * o:BY + 512 * o + 24], [h])
+        dma("y" if o == 0 else "s", "o1" if o == 0 else "o2", [h], T.y[:, 168 * o + 144:168 * o + 168], T.yo[:, 168 * o + 144:168 * o + 168])
+    wait("g", [(k, count[k]) for k in ("v", "s", "p", "g", "loc", "o1", "o2")])

@@ -17,8 +17,8 @@ A = AluOpType
 COPY = ActivationFunctionType.Copy
 LOW = -1e29
 BG, BR, BY, BD = 0, 512, 1024, 2048
-ORDER = ("s0 m1 s1 m2 c1-3 s2 p1-2 m3 x1 s3 k1 m4 x2 c4-7 s4 k2 p3-4 m5 x3 s5 k3 m6 x4 c8-11 s6 k4 p5-6 m7 x5 s7 k5 "
-         "c12-14 x6 p7 k6 x7 k7").split()
+ORDER = ("s0 m1 n1 s1 p1 m2 x1 s2 c2-3 m3 k1 p2 s3 c4-5 x2 m4 p3 k2 s4 c6-7 x3 m5 p4 k3 s5 c8-9 x4 m6 p5 k4 c10-11 s6 x5 p6 m7 k5 "
+         "c12 n7 x6 s7 p7 k6 c14 x7 k7").split()
 
 
 def fit(vals, dims):
@@ -136,6 +136,16 @@ def rank_program(g, core, T, topo):
     LG, LO, LA, LY = 0, 8, [18, 50, 78], [84, 90]
     OO = [0, 32, 64]
 
+    def keys(L, deps):
+        v, c = WO[L], LA[L]
+        for p in pcs[L]:
+            n = len(p["key"])
+            iota(T.key[:, v:v + n], p["key"], p["dims"], deps=deps)
+            hk = iota(T.ct[:, c:c + n // 4], [4 * s for s in p["src"][0::4]], p["dims"][:-1] + ([2] if p["dims"][-1] == 8 else []))
+            v += n
+            c += n // 4
+        return hk
+
     hx = dma("y", "ldx", [], T.xt[:], T.x[:])
     hw = dma("y", "ldw", [], T.wt[:], T.w[:])
 
@@ -150,21 +160,21 @@ def rank_program(g, core, T, topo):
         hct = iota(T.ct[:, LO:LO + 8], [8 + 32 * c for c in range(8)], [8])
         nG, nO = 96, 128
     hid = op("g", [hones], lambda: g.affine_select(T.ident[:], T.ones[:], [[-1, 128]], A.is_equal, 0.0, 0, 1))
-    hu64 = op("g", [hones], lambda: g.affine_select(T.u64[:], T.ones[:, 0:64], [[1, 4], [0, 4], [-1, 4]], A.is_equal, 0.0, 0, 0))
     hi4 = iota(T.i4[:], [0, 1, 2, 3], [4])
+    hkey = [keys(0, [])]
     for k, (sh, mk) in enumerate([(0, 15), (0, 7), (3, 1), (2, 3), (0, 3), (0, 127)]):
         hj = ts(T.pj[:, k:k + 1], T.pi[:], sh, A.logical_shift_right, mk, A.bitwise_and, deps=[hp])
     hdg = mset(T.dg[:], 0.0)
     hpf = cp(T.pf[:, 0:6], T.pj[:, 0:6], [hj])
     p16, p8, ph, p4, pq, pp = [T.pf[:, k:k + 1] for k in range(6)]
     mset(T.cs[:, 0, 0:1], 4.0)
+    mset(T.cs[:, 0, 1:16:2], 1.0 - 2.0 ** -22)
     if b0 == 0:
         h = ts(T.rt[:, 0:1], p16, 11.0, A.min, 16.0, A.mult, deps=[hpf])
     else:
         h = ts(T.rt[:, 0:1], ph, 16.0, A.mult, p8, A.add, deps=[hpf])
-    mset(T.cs[:, 0, 1:16:2], 1.0 - 2.0 ** -22)
-    hl = ts(T.ls[:, 0:LO + nO // 16], T.ct[:, 0:LO + nO // 16], T.rt[:, 0:1], A.add, 191.0, A.min, deps=[h, hct])
     hz = quant("l0", 96 if b0 == 0 else 128, 128, T.dg[:, 304:816], [hdg])
+    hl = ts(T.ls[:, 0:LO + nO // 16], T.ct[:, 0:LO + nO // 16], T.rt[:, 0:1], A.add, 191.0, A.min, deps=[h, hct])
 
     for i in range(8):
         hpw = act(T.pwn[:, i:96:8], T.ones[:, 0:12], 8.0 ** (8 - i) if i else 0.0, deps=[hones])
@@ -195,28 +205,19 @@ def rank_program(g, core, T, topo):
     count["loc"] += 2 * half
     ha1 = ("a1", len(topo.engines(mate, core)) // 2 * 2)
 
+    hu64 = op("g", [hones], lambda: g.affine_select(T.u64[:], T.ones[:, 0:64], [[1, 4], [0, 4], [-1, 4]], A.is_equal, 0.0, 0, 0))
     hoc, hos = pick("o", nO, LO)
     for b in range(4):
         hqe = quant("e", 128 * b, 128, T.et[:, 3 - b:515 - b], [he])
     mset(T.z[:], LOW)
     for i in range(8):
         hpb = act(T.pwb[:, 8 * i:8 * i + 8], T.ones[:, 0:8], 8.0 ** (8 - i) if i else 0.0)
-    hkey = []
     for L in range(3):
-        v, c = WO[L], LA[L]
+        v = WO[L]
         for p in pcs[L]:
-            n = len(p["key"])
-            iota(T.key[:, v:v + n], p["key"], p["dims"], deps=[("g", count["g"])] if (L, v) == (1, WO[1]) else [])
-            hk = iota(T.ct[:, c:c + n // 4], [4 * s for s in p["src"][0::4]], p["dims"][:-1] + ([2] if p["dims"][-1] == 8 else []))
-            v += n
-            c += n // 4
-        hkey.append(hk)
-        if L == 0:
-            for L2 in range(3):
-                v = WO[L2]
-                for p in pcs[L2]:
-                    hb = iota(T.dg[96:97, v:v + len(p["key"])], p["base"], p["dims"], deps=[hdg, hk])
-                    v += len(p["key"])
+            hb = iota(T.dg[96:97, v:v + len(p["key"])], p["base"], p["dims"], deps=[hdg, hu64])
+            v += len(p["key"])
+    hkey += [keys(1, [hb]), keys(2, [])]
     iota(T.ct[:, LY[0]:LY[0] + 6], [(4 * (c ^ b2) + a) if b1 == 0 else (24 * (c ^ b2) + 8 * a) for a in range(3) for c in range(2)], [3, 2])
     hcy = iota(T.ct[:, LY[1]:LY[1] + 3], [m if b2 == 0 else 88 + 8 * m for m in range(3)], [3])
 
@@ -232,13 +233,8 @@ def rank_program(g, core, T, topo):
         free["d"] = h
         return h
     decode_cp(decode_mm(("o", 0, 128), [hoc, hos]), "d0", [(0, 128, 128 if b0 == 0 else 0)])
-    h = act(T.ut[:, 0:64], T.u64[:], 4.0, deps=[hu64])
     for i in range(1, 8):
         hcd = act(T.wr[:, i, :], T.ones[:, 0:8], 1.0 + 8.0 ** (i - 8))
-        if i in (2, 4, 6):
-            n = 32 << (i // 2)
-            h = act(T.ut[:, n:2 * n], T.ut[:, 0:n], deps=[h])
-    hut = h
     rts = {}
 
     def tables(L, quads):
@@ -250,8 +246,8 @@ def rank_program(g, core, T, topo):
                 k = 1 + len(rts)
                 rts[gam] = (T.rt[:, k:k + 1], ts(T.rt[:, k:k + 1], p4, float(gam), A.mult, pq, A.add, deps=[hpf]))
         v, n = WO[L], ncol[L]
-        cp(T.wd[:, v + n:v + n + 8], T.pwn[:, 0:8], [hpw])
         heq = ts(T.key[:, v:v + n], T.key[:, v:v + n], pp, A.is_equal, deps=[hkey[L]])
+        cp(T.wd[:, v + n:v + n + 8], T.pwn[:, 0:8], [hpw])
         c = LA[L]
         for p, gam in zip(pcs[L], gams):
             m = len(p["key"]) // 4
@@ -262,11 +258,14 @@ def rank_program(g, core, T, topo):
             hwd = tt(T.wd[:, v:v + m], T.key[:, v:v + m], T.pwb[:, 0:m] if p["kind"] == "blk" else T.pwn[:, 0:m], A.mult, deps=[heq, hpw, hpb])
             v += m
         return hla, hwd
+    tab = [tables(0, [(0, 0), (1, 36), (2, 72)]), None, None]
     if b1 == 1:
         mset(T.mt[:, 928:1056], 0.0)
         quant("m0", 128, 128, T.dg[:, 304:816], [hdg])
-    tab = [tables(0, [(0, 0), (1, 36), (2, 72)]), None, None]
-    hqu = quant("u", 0, 128, T.ut[:], [hut])
+    h = ts(T.ut[:, 0:64], T.u64[:], 4.0, A.mult, deps=[hu64])
+    for k in range(1, 8):
+        h = ts(T.ut[:, 64 * k:64 * k + 64], T.u64[:], 4.0, A.mult)
+    hqu = quant("u", 0, 128, T.ut[:], [h])
 
     def level(L, lo, hi, prods, deps, dec, runs, dcols, mid=None):
         n, v = ncol[L], WO[L]
@@ -300,10 +299,10 @@ def rank_program(g, core, T, topo):
                 hc = tt(cd[lo:hi, i:j + 1, 0:16:2], z[lo:hi, i:j + 1, 3:32:4], z[lo:hi, i - 1:j, 3:32:4], A.is_le, deps=[done[j]])
                 for row in range(i, j + 1):
                     done["c", row] = hc
+            elif k == "n":
+                done["c", 2 * i - 1] = tt(cd[lo:hi, 2 * i - 1, 0:16:2], z[lo:hi, 2 * i - 2, 7:36:4], z[lo:hi, 2 * i - 2, 3:32:4], A.is_le, deps=[done[2 * i - 2]])
             elif k == "p":
-                hc = tt(cd[lo:hi, 2 * i - 1:2 * j:2, 1:16:2], T.wr[lo:hi, i:j + 1, :], cd[lo:hi, 2 * i - 1:2 * j:2, 0:16:2], A.subtract, deps=[done["c", 2 * j - 1], hcd])
-                for row in range(i, j + 1):
-                    done["p", row] = hc
+                done["p", i] = tt(cd[lo:hi, 2 * i - 1, 1:16:2], T.wr[lo:hi, i, :], cd[lo:hi, 2 * i - 1, 0:16:2], A.subtract, deps=[done["c", 2 * i - 1], hcd])
             elif k == "x":
                 done["x", i] = tt(cs[lo:hi, i - 1, 2:16:2], cs[lo:hi, i - 1, 1:14:2], cd[lo:hi, 2 * i - 1, 3:16:2], A.add, deps=[done["p", i], done.get(("k", i - 1))])
             else:
@@ -357,13 +356,13 @@ def rank_program(g, core, T, topo):
     hp8 = ts(T.rt[:, 12:13], p8, 8.0, A.mult, deps=[hpf])
     if b2 == 0:
         mset(T.mt[:, 448:544], 0.0)
+    tab[1] = tables(1, [(0, -1), (1, 36), (2, 67)])
     h0 = ts(T.rt[:, 13:14], ph, 64.0 if b1 == 0 else 48.0, A.mult, T.rt[:, 12:13] if b1 == 0 else p8, A.add, deps=[hp8])
     h1 = ts(T.rt[:, 14:15], ph, 4.0 if b2 == 0 else -24.0, A.mult, T.rt[:, 12:13] if b2 == 0 else p8, A.add, deps=[hp8])
+    tab[2] = tables(2, [(2, 64)])
     ts(T.ls[:, LY[0]:LY[0] + 6], T.ct[:, LY[0]:LY[0] + 6], T.rt[:, 13:14], A.add, deps=[h0, hcy])
     hly = ts(T.ls[:, LY[1]:LY[1] + 3], T.ct[:, LY[1]:LY[1] + 3], T.rt[:, 14:15], A.add, deps=[h1, hcy])
     outputs(0, hm0, hqw, hly, 0, 96)
-    tab[1] = tables(1, [(0, -1), (1, 36), (2, 67)])
-    tab[2] = tables(2, [(2, 64)])
 
     if b1 == 0:
         prods, runs = [(("l1", 56), ("m0", 0, 128)), (("l1", 184), ("l1", 0, 128))], [(256, 24, cB2), (0, 112, cA2)]

@@ -8,17 +8,20 @@ for _n, _w in dict(x=192, w=256, g=128, o=144, l0=256, l1=320, m0=256, m1=128, m
 for _d, _b in {"bfloat16": dict(xt=[768], wt=[1024], et=[516], ut=[512], ones=[128], ident=[128], u64=[64], dg=[816], mt=[1056],
                                 d0=[1024], d1=[800], d2=[352], am0=[512], am1=[448], am2=[96]),
                "int32": dict(pi=[1], pj=[8], fa=[136], fb=[136]), "uint16": dict(ls=[128], off=[96]),
-               "float32": dict(pf=[8], rt=[16], ct=[128], i4=[4], m4=[12], key=[304], wd=[304], pwn=[96], pwb=[64], tt=[8, 32], gs=[8, 32],
-                               z=[16, 36], cs=[8, 16], cd=[16, 16], wr=[8, 8], ptf=[24], yt=[512], yo=[336])}.items():
+               "float32": dict(pf=[8], rt=[16], ct=[128], i8=[8], m4=[8], wd=[304], pwn=[96], pwb=[64], tt=[8, 32], ge=[40, 4], go=[48, 4],
+                               z=[9, 272], cs=[8, 96], cd=[8, 28], wj=[8, 8], ptf=[24], yt=[512], yo=[336])}.items():
     for _n, _w in _b.items():
         SCRATCH[_n] = ("sbuf", [128] + _w, _d)
 SEMAPHORES = ["v", "s", "p", "g", "ldx", "ldw", "a1", "a2", "loc", "o1", "o2"]
 A = AluOpType
 COPY = ActivationFunctionType.Copy
 LOW = -1e29
+FIRST = -2.0 ** -22
 BG, BR, BY, BD = 0, 512, 1024, 2048
-ORDER = ("s0 m1 n1 s1 p1 m2 x1 s2 c2-3 m3 k1 p2 s3 c4-5 x2 m4 p3 k2 s4 c6-7 x3 m5 p4 k3 s5 c8-9 x4 m6 p5 k4 c10-11 s6 x5 p6 m7 k5 "
-         "c12 n7 x6 s7 p7 k6 c14 x7 k7").split()
+ZQ, ZK, ZO, ZP, ZA = 20, [5, 6], [(6, 31), (1, 25)], [30, 26], 6
+CQ, CK, CO = 4, [4, 3], [(3, 7), (5, 8)]
+ORDER = ("e1 S0 s0 e0 s1 S1 b1 s2 S2 a1 b2 S3 s3 a2 K1 k1 S4 s4 K2 k2 s5 b4 S5 b3-5 a3-5 a4 s6 K3 k3 a6 S6 K4 k4 s7 b6 k5 K5 "
+         "a7 b7 k6 K6 k7").split()
 
 
 def fit(vals, dims):
@@ -136,19 +139,32 @@ def rank_program(g, core, T, topo):
     LG, LO, LA, LY = 0, 8, [18, 50, 78], [84, 90]
     OO = [0, 32, 64]
 
-    def keys(L, deps):
-        v, c = WO[L], LA[L]
+    def terms(L, deps):
+        c = LA[L]
         for p in pcs[L]:
             n = len(p["key"])
-            iota(T.key[:, v:v + n], p["key"], p["dims"], deps=deps)
-            hk = iota(T.ct[:, c:c + n // 4], [4 * s for s in p["src"][0::4]], p["dims"][:-1] + ([2] if p["dims"][-1] == 8 else []))
-            v += n
+            hk = iota(T.ct[:, c:c + n // 4], [4 * s for s in p["src"][0::4]], p["dims"][:-1] + ([2] if p["dims"][-1] == 8 else []), deps=deps)
             c += n // 4
         return hk
 
-    hx = dma("y", "ldx", [], T.xt[:], T.x[:])
-    hw = dma("y", "ldw", [], T.wt[:], T.w[:])
+    def weights(L, deps):
+        v = WO[L]
+        for p in pcs[L]:
+            n = len(p["key"])
+            pat, base = fit(p["key"], p["dims"])
+            src = T.pwb[:, 0:n] if p["kind"] == "blk" else T.pwn[:, 0:n]
+            hk = op("g", deps, lambda: g.affine_select(T.wd[:, v:v + n], src, pat, A.is_equal, 0.0, base, -1))
+            v += n
+        return hk
 
+    def bases(L, deps):
+        v = WO[L]
+        for p in pcs[L]:
+            hk = iota(T.dg[96:97, v:v + len(p["key"])], p["base"], p["dims"], deps=deps)
+            v += len(p["key"])
+        return hk
+
+    hx = dma("y", "ldx", [], T.xt[:], T.x[:])
     hones = mset(T.ones[:], 1.0)
     hp = op("g", [], lambda: g.iota(T.pi[:], [[0, 1]], 0, 1))
     if b0 == 0:
@@ -160,66 +176,78 @@ def rank_program(g, core, T, topo):
         hct = iota(T.ct[:, LO:LO + 8], [8 + 32 * c for c in range(8)], [8])
         nG, nO = 96, 128
     hid = op("g", [hones], lambda: g.affine_select(T.ident[:], T.ones[:], [[-1, 128]], A.is_equal, 0.0, 0, 1))
-    hi4 = iota(T.i4[:], [0, 1, 2, 3], [4])
-    hkey = [keys(0, [])]
+    hi8 = iota(T.i8[:], list(range(8)), [8])
+    hu64 = op("g", [hones], lambda: g.affine_select(T.u64[:], T.ones[:, 0:64], [[1, 4], [0, 4], [-1, 4]], A.is_equal, 0.0, 0, 0))
+    hterm = [terms(0, [])]
+    hdg = mset(T.dg[:], 0.0)
     for k, (sh, mk) in enumerate([(0, 15), (0, 7), (3, 1), (2, 3), (0, 3), (0, 127)]):
         hj = ts(T.pj[:, k:k + 1], T.pi[:], sh, A.logical_shift_right, mk, A.bitwise_and, deps=[hp])
-    hdg = mset(T.dg[:], 0.0)
+    mset(T.ge[:, 0:40:5, :], 0.0)
+    mset(T.go[:, 0:48:6, :], 0.0)
     hpf = cp(T.pf[:, 0:6], T.pj[:, 0:6], [hj])
     p16, p8, ph, p4, pq, pp = [T.pf[:, k:k + 1] for k in range(6)]
-    mset(T.cs[:, 0, 0:1], 4.0)
-    mset(T.cs[:, 0, 1:16:2], 1.0 - 2.0 ** -22)
+    mset(T.go[:, 1:48:6, :], 0.0)
+    mset(T.cd[:, 2:8:2, 2:28:4], 0.0)
     if b0 == 0:
         h = ts(T.rt[:, 0:1], p16, 11.0, A.min, 16.0, A.mult, deps=[hpf])
     else:
         h = ts(T.rt[:, 0:1], ph, 16.0, A.mult, p8, A.add, deps=[hpf])
-    hz = quant("l0", 96 if b0 == 0 else 128, 128, T.dg[:, 304:816], [hdg])
+    mset(T.cs[:, 1:8, CQ:CQ + 1], FIRST)
+    mset(T.cs[:, 0, CQ:CQ + 84:12], FIRST)
     hl = ts(T.ls[:, 0:LO + nO // 16], T.ct[:, 0:LO + nO // 16], T.rt[:, 0:1], A.add, 191.0, A.min, deps=[h, hct])
 
     for i in range(8):
-        hpw = act(T.pwn[:, i:96:8], T.ones[:, 0:12], 8.0 ** (8 - i) if i else 0.0, deps=[hones])
+        hpw = act(T.pwn[:, i:96:8], T.ones[:, 0:12], -8.0 ** (8 - i) if i else 0.0, deps=[hones])
+    for i in range(8):
+        hpb = act(T.pwb[:, 8 * i:8 * i + 8], T.ones[:, 0:8], -8.0 ** (8 - i) if i else 0.0)
     for e in range(4):
         act(T.et[:, e:512:4], T.ident[:], 1.0 if e == 3 else 0.0, deps=[hid])
     he = act(T.et[:, 512:516], T.ones[:, 0:4], 0.0)
     for i in range(1, 8):
-        act(T.cd[:, 2 * i, 1:16:2], T.ones[:, 0:8], -sum(8.0 ** (k - 8) for k in range(1, i + 1)))
+        hwj = act(T.wj[:, :, i], T.i8[:], -8.0 ** (i - 8), deps=[hi8])
 
     hqx = quant("x", 0, 192, T.xt[:], [hx])
 
-    def pick(b, n, lst):
+    def pick(b, n, lst, scales):
         o = T.ls[:, lst:lst + n // 16]
         hc = cp(T["q" + b][:, 0:n].bitcast(dt.uint32), T.qx[:, 0:192].bitcast(dt.uint32).indirect(o), [hqx, hl])
-        return hc, gat(T["s" + b][:, 0:n], T.sx[:, 0:192].indirect(o), [hqx, hl])
-    hgc, hgs = pick("g", nG, LG)
+        return hc, scales(T["s" + b][:, 0:n], T.sx[:, 0:192].indirect(o), [hqx, hl])
+    hgc, hgs = pick("g", nG, LG, cp)
 
     def bits(es):
         return sum(1 << e for e in es)
     mate = T.cores[r ^ 1]
     rid, pid = topo.addr(mate, core)
     es = topo.engines(core, mate)
-    half = len(es) // 2
     wait("g", [hgc])
-    g.remote_dma(T.ql0[:, 0:nG].bitcast(dt.uint8), T.qg[:, 0:nG].bitcast(dt.uint8), T.sem.a1, T.sem.loc, pid, rid, bits(es[:half]))
+    g.remote_dma(T.ql0[:, 0:nG].bitcast(dt.uint8), T.qg[:, 0:nG].bitcast(dt.uint8), T.sem.a1, T.sem.loc, pid, rid, bits(es))
     wait("g", [hgs])
-    g.remote_dma(T.sl0[:, 0:nG], T.sg[:, 0:nG], T.sem.a1, T.sem.loc, pid, rid, bits(es[half:]))
-    count["loc"] += 2 * half
-    ha1 = ("a1", len(topo.engines(mate, core)) // 2 * 2)
-
-    hu64 = op("g", [hones], lambda: g.affine_select(T.u64[:], T.ones[:, 0:64], [[1, 4], [0, 4], [-1, 4]], A.is_equal, 0.0, 0, 0))
-    hoc, hos = pick("o", nO, LO)
-    for b in range(4):
-        hqe = quant("e", 128 * b, 128, T.et[:, 3 - b:515 - b], [he])
-    mset(T.z[:], LOW)
-    for i in range(8):
-        hpb = act(T.pwb[:, 8 * i:8 * i + 8], T.ones[:, 0:8], 8.0 ** (8 - i) if i else 0.0)
-    for L in range(3):
-        v = WO[L]
-        for p in pcs[L]:
-            hb = iota(T.dg[96:97, v:v + len(p["key"])], p["base"], p["dims"], deps=[hdg, hu64])
-            v += len(p["key"])
-    hkey += [keys(1, [hb]), keys(2, [])]
+    g.remote_dma(T.sl0[:, 0:nG], T.sg[:, 0:nG], T.sem.a1, T.sem.loc, pid, rid, bits(es))
+    count["loc"] += 2 * len(es)
+    ha1 = ("a1", 2 * len(topo.engines(mate, core)))
+    hw = dma("y", "ldw", [ha1], T.wt[:], T.w[:])
+    hwd = [weights(0, [hpw, hpb])]
+    hb = [bases(0, [hdg, hwd[0]])]
+    hb.append(bases(1, []))
+    hb.append(bases(2, []))
+    hterm += [terms(1, [hb[2]]), terms(2, [])]
+    hwd += [weights(1, []), weights(2, [])]
     iota(T.ct[:, LY[0]:LY[0] + 6], [(4 * (c ^ b2) + a) if b1 == 0 else (24 * (c ^ b2) + 8 * a) for a in range(3) for c in range(2)], [3, 2])
     hcy = iota(T.ct[:, LY[1]:LY[1] + 3], [m if b2 == 0 else 88 + 8 * m for m in range(3)], [3])
+
+    hoc, hos = pick("o", nO, LO, gat)
+    for b in range(4):
+        hqe = quant("e", 128 * b, 128, T.et[:, 3 - b:515 - b], [he])
+    hz = quant("l0", 96 if b0 == 0 else 128, 128, T.dg[:, 304:816], [hdg])
+    h = mset(T.z[:, 0:8:2, ZQ:ZQ + 240:6], LOW)
+    mset(T.z[:, 1:8:2, ZQ:ZQ + 240:5], LOW)
+    mset(T.cs[:, 1:8:2, CQ + 3:CQ + 84:3], 8.0)
+    mset(T.cs[:, 0:8:2, CQ + 4:CQ + 84:12], 8.0)
+    mset(T.cs[:, 0, CQ + 8:CQ + 84:12], FIRST)
+    mset(T.z[:, 0, ZQ + 6:ZQ + 7], 0.0, [h])
+    cp(T.cd[:, 1:8:2, 1:21:3], T.wj[:, 1:8:2, 1:8], [hwj])
+    cp(T.cd[:, 2:8:2, 1:28:4], T.wj[:, 2:8:2, 1:8], [hwj])
+    ts(T.m4[:, 0:4], T.i8[:, 0:4], pq, A.is_equal, deps=[hi8, hpf])
 
     free = {"d": None, "y": None}
 
@@ -232,85 +260,82 @@ def rank_program(g, core, T, topo):
                 h = act(T[dst][:, 4 * at + b:4 * (at + n):4], T.ps[:, BD + 512 * b + a:BD + 512 * b + a + n], 0.5, deps=[hs[b]])
         free["d"] = h
         return h
+    for k in range(8):
+        hut = act(T.ut[:, 64 * k:64 * k + 64], T.u64[:], 4.0, deps=[hu64])
     decode_cp(decode_mm(("o", 0, 128), [hoc, hos]), "d0", [(0, 128, 128 if b0 == 0 else 0)])
-    for i in range(1, 8):
-        hcd = act(T.wr[:, i, :], T.ones[:, 0:8], 1.0 + 8.0 ** (i - 8))
+    for L in range(3):
+        hw8 = act(T.wd[:, WO[L] + ncol[L]:WO[L] + ncol[L] + 8], T.pwn[:, 0:8], deps=[hpw])
     rts = {}
 
-    def tables(L, quads):
-        for a, c in quads:
-            ts(T.m4[32 * a:32 * a + 32, 4 * L:4 * L + 4], T.i4[32 * a:32 * a + 32, :], float(c), A.add, T.pf[32 * a:32 * a + 32, 5:6], A.is_equal, deps=[hi4, hpf])
+    def tables(L):
         gams = [4 * (p["src"][1] - p["src"][0]) for p in pcs[L]]
         for gam in gams:
             if gam not in rts:
                 k = 1 + len(rts)
                 rts[gam] = (T.rt[:, k:k + 1], ts(T.rt[:, k:k + 1], p4, float(gam), A.mult, pq, A.add, deps=[hpf]))
-        v, n = WO[L], ncol[L]
-        heq = ts(T.key[:, v:v + n], T.key[:, v:v + n], pp, A.is_equal, deps=[hkey[L]])
-        cp(T.wd[:, v + n:v + n + 8], T.pwn[:, 0:8], [hpw])
         c = LA[L]
         for p, gam in zip(pcs[L], gams):
             m = len(p["key"]) // 4
-            hla = ts(T.ls[:, c:c + m], T.ct[:, c:c + m], rts[gam][0], A.add, deps=[rts[gam][1], hkey[L]])
+            hla = ts(T.ls[:, c:c + m], T.ct[:, c:c + m], rts[gam][0], A.add, deps=[rts[gam][1], hterm[L]])
             c += m
-        for p in pcs[L]:
-            m = len(p["key"])
-            hwd = tt(T.wd[:, v:v + m], T.key[:, v:v + m], T.pwb[:, 0:m] if p["kind"] == "blk" else T.pwn[:, 0:m], A.mult, deps=[heq, hpw, hpb])
-            v += m
-        return hla, hwd
-    tab = [tables(0, [(0, 0), (1, 36), (2, 72)]), None, None]
+        return hla
+    tab = [tables(0), None, None]
     if b1 == 1:
         mset(T.mt[:, 928:1056], 0.0)
         quant("m0", 128, 128, T.dg[:, 304:816], [hdg])
-    h = ts(T.ut[:, 0:64], T.u64[:], 4.0, A.mult, deps=[hu64])
-    for k in range(1, 8):
-        h = ts(T.ut[:, 64 * k:64 * k + 64], T.u64[:], 4.0, A.mult)
-    hqu = quant("u", 0, 128, T.ut[:], [h])
+    hqu = quant("u", 0, 128, T.ut[:], [hut])
 
     def level(L, lo, hi, prods, deps, dec, runs, dcols, mid=None):
         n, v = ncol[L], WO[L]
-        hla, hwd = tab[L]
         dw, am = T["d%d" % L][:, 0:4 * dcols], T["am%d" % L][:, 0:4 * n]
         for k, (st, mv) in enumerate(prods):
             hg = mm(BG, st, mv, k == 0, k == len(prods) - 1, deps)
         hs = decode_mm(dec, deps)
         nt = 2 if L == 0 else 4
         for k in range(nt):
-            ht = op("v", [hg], lambda: V.transpose(T.tt[lo:hi, 8 // nt * k:8 // nt * (k + 1), :], T.ps[lo:hi, BG + 32 // nt * k:BG + 32 // nt * k + 256 // nt]))
-        at = [8 // nt * (i % nt) + i // nt for i in range(8)]
-        for s in (2, 3):
-            hb2 = act(T.gs[lo:hi, :, s:32:4], T.tt[lo:hi, :, 8 * s:8 * s + 8], T.m4[lo:hi, 4 * L + s:4 * L + s + 1], deps=[ht])
-        for s in (0, 1):
-            h = ts(T.gs[lo:hi, :, s:32:4], T.tt[lo:hi, :, 8 * s:8 * s + 8], T.m4[lo:hi, 4 * L + s:4 * L + s + 1], A.mult, deps=[ht])
+            ht = op("v", [hg], lambda: V.transpose(T.tt[lo:hi, k:8:nt, :], T.ps[lo:hi, BG + 32 // nt * k:BG + 32 // nt * k + 256 // nt]))
+        gs = [T.ge, T.go]
+
+        def mask(f, par, s):
+            c = 4 * (L % 2) + s
+            o, i, m = gs[par][lo:hi, 1 + par + s:8 * ZK[par]:ZK[par], :], T.tt[lo:hi, :, 8 * s + par:8 * s + 8:2], T.m4[lo:hi, c:c + 1]
+            return act(o, i, m, deps=[ht]) if f == "s" else ts(o, i, m, A.mult, deps=[ht])
+        ready = [[mask("s", 0, s) for s in (2, 3)] + [mask("v", 0, s) for s in (0, 1)], [mask("s", 1, s) for s in (2, 3)]]
         hd = decode_cp(hs, "d%d" % L, runs)
-        ham = gat(am, dw.indirect(T.ls[:, LA[L]:LA[L] + n // 4]), [hd, hla])
+        ham = gat(am, dw.indirect(T.ls[:, LA[L]:LA[L] + n // 4]), [hd, tab[L]])
         if mid is not None:
             mid()
         z, cs, cd = T.z, T.cs, T.cd
         done = {}
         for tok in ORDER:
-            k, i, j = tok[0], int(tok[1:].split("-")[0]), int(tok[1:].split("-")[-1])
-            if k == "s":
-                done[2 * i] = scan(z[lo:hi, 2 * i, 4:36], z[lo:hi, (2 * i - 1) % 16, 3:35], T.gs[lo:hi, at[i], :], LOW if i else 0.0,
-                                   A.max, A.add, [done[2 * i - 1]] if i else [h, hb2])
-            elif k == "m":
-                done[2 * i - 1] = tt(z[lo:hi, 2 * i - 1, 3:32:4], z[lo:hi, 2 * i - 2, 3:32:4], z[lo:hi, 2 * i - 2, 7:36:4], A.max, deps=[done[2 * i - 2]])
-            elif k == "c":
-                hc = tt(cd[lo:hi, i:j + 1, 0:16:2], z[lo:hi, i:j + 1, 3:32:4], z[lo:hi, i - 1:j, 3:32:4], A.is_le, deps=[done[j]])
-                for row in range(i, j + 1):
-                    done["c", row] = hc
-            elif k == "n":
-                done["c", 2 * i - 1] = tt(cd[lo:hi, 2 * i - 1, 0:16:2], z[lo:hi, 2 * i - 2, 7:36:4], z[lo:hi, 2 * i - 2, 3:32:4], A.is_le, deps=[done[2 * i - 2]])
-            elif k == "p":
-                done["p", i] = tt(cd[lo:hi, 2 * i - 1, 1:16:2], T.wr[lo:hi, i, :], cd[lo:hi, 2 * i - 1, 0:16:2], A.subtract, deps=[done["c", 2 * i - 1], hcd])
-            elif k == "x":
-                done["x", i] = tt(cs[lo:hi, i - 1, 2:16:2], cs[lo:hi, i - 1, 1:14:2], cd[lo:hi, 2 * i - 1, 3:16:2], A.add, deps=[done["p", i], done.get(("k", i - 1))])
+            k, j, e = tok[0], int(tok[1:].split("-")[0]), int(tok[1:].split("-")[-1])
+            par = j % 2
+            if k == "e":
+                ready[1].append(mask("v", 1, j))
+            elif k in "sS":
+                o, st = ZO[par][k == "S"], 30 // ZK[par]
+                done[k, j] = scan(z[lo:hi, j + 1, o:o + 240:st], z[lo:hi, j, ZQ:ZQ + 240:st], gs[par][lo:hi, :, j // 2], LOW, A.max, A.add,
+                                  [done.get(("s", j - 1)), done.get(("S", j - 1))] + ready[par])
+            elif k in "kK":
+                o, st = CO[par][k == "K"], 12 // CK[par]
+                done[k, j] = scan(cs[lo:hi, j, o:o + 84:st], cd[lo:hi, j, 0:7 * CK[par]], cs[lo:hi, j - 1, CQ:CQ + 84:st], FIRST, A.add, A.min,
+                                  [done["a", j], done["b", j], done.get(("k", j - 1)), done.get(("K", j - 1))])
             else:
-                done["k", i] = scan(cs[lo:hi, i, :], cd[lo:hi, 2 * i, :], cs[lo:hi, i - 1, :], 4.0, A.add, A.min, [done["x", i], done["c", 2 * i]])
-        h = ts(T.fa[lo:hi, 0:n + 8], T.wd[lo:hi, v:v + n + 8], cs[lo:hi, 7, 15:16], A.mult, -0.5, A.add, deps=[done["k", 7], hwd])
-        h = ts(T.fb[lo:hi, 0:n + 8], T.fa[lo:hi, 0:n + 8], 7, A.bitwise_and, deps=[h])
-        hdig = cp(T.dg[lo:hi, v:v + n + 8], T.fb[lo:hi, 0:n + 8], [h])
-        h = quant("d", 0, 128, T.dg[:, v:v + 512], [hdig, hb])
+                c, was, now = CK[par], ZP[1 - par], ZP[par]
+                if k == "a":
+                    hc = tt(cd[lo:hi, j:e + 1:2, 0:7 * c:c], z[lo:hi, j:e + 1:2, was:was + 210:30], z[lo:hi, j + 1:e + 2:2, now:now + 210:30],
+                            A.is_ge, deps=[done["s", e]])
+                else:
+                    hc = tt(cd[lo:hi, j:e + 1:2, c - 1:7 * c:c], z[lo:hi, j:e + 1:2, was + 30:was + 240:30], z[lo:hi, j + 1:e + 2:2, ZA + 30:ZA + 240:30],
+                            A.is_gt, deps=[done["s", e]])
+                for col in range(j, e + 1, 2):
+                    done[k, col] = hc
+        last = CO[1][0] + 80
+        cuts = [(0, n + 8)] if n < 64 else [(0, n // 2), (n // 2, n + 8)]
+        h = [ts(T.fa[lo:hi, a:b], T.wd[lo:hi, v + a:v + b], cs[lo:hi, 7, last:last + 1], A.mult, -0.5, A.add, deps=[done["k", 7], hwd[L], hw8]) for a, b in cuts]
+        h = [ts(T.fb[lo:hi, a:b], T.fa[lo:hi, a:b], 7, A.bitwise_and, deps=[d]) for (a, b), d in zip(cuts, h)]
+        hdig = [cp(T.dg[lo:hi, v + a:v + b], T.fb[lo:hi, a:b], [d]) for (a, b), d in zip(cuts, h)][-1]
+        h = quant("d", 0, 128, T.dg[:, v:v + 512], [hdig, hb[2]])
         hpt = act(T.ptf[lo:hi, 8 * L:8 * L + 8], T.dg[lo:hi, v + n:v + n + 8], deps=[hdig])
         h = mm(BR, ("u", 0), ("d", 0, 128), True, True, [h, hqu])
         o = T.off[:, OO[L]:OO[L] + n // 4]
@@ -325,7 +350,7 @@ def rank_program(g, core, T, topo):
         for o in range(2):
             w0, y0 = 256 * L + 128 * o, 168 * o + at
             h = gat(T.yo[:, y0:y0 + n], T.yt[:, w0:w0 + 128].indirect(T.ls[:, LY[L]:LY[L] + n // 16]), [hc[o], hly])
-            dma("y", "o1", [h], T.y[:, y0:y0 + n], T.yo[:, y0:y0 + n])
+            dma("y", "o1", [h, ha2], T.y[:, y0:y0 + n], T.yo[:, y0:y0 + n])
 
     prods = [(("l0", 0), ("o", 0, 144))] if b0 == 0 else [(("o", 0), ("l0", 0, 144))]
     hm0, hpt = level(0, 0, 96, prods, [ha1, hz, hoc, hos], ("l0", 0, 128), [(0, 128, 128 * b0)], 256)
@@ -348,7 +373,7 @@ def rank_program(g, core, T, topo):
     count["loc"] += 8 * k4
     ha2 = ("a2", 8 * k4)
     for a in range(3):
-        dma("y", "o1", [hpt], T.pt[0:1, 32 * a:32 * a + 32], T.ptf[36 * a:36 * a + 4, 0:8])
+        dma("y", "o1", [hpt, ha2], T.pt[0:1, 32 * a:32 * a + 32], T.ptf[36 * a:36 * a + 4, 0:8])
 
     decode_cp(decode_mm(("m0", 0, 128), [hm0]), "d1", [(0, 64, cA1)] if b1 == 0 else [(48, 48, cB1)])
     hqw = quant("w", 0, 256, T.wt[:], [hw])
@@ -356,10 +381,12 @@ def rank_program(g, core, T, topo):
     hp8 = ts(T.rt[:, 12:13], p8, 8.0, A.mult, deps=[hpf])
     if b2 == 0:
         mset(T.mt[:, 448:544], 0.0)
-    tab[1] = tables(1, [(0, -1), (1, 36), (2, 67)])
+    for a, c in [(0, -1), (1, 36), (2, 67)]:
+        ts(T.m4[32 * a:32 * a + 32, 4:8], T.i8[32 * a:32 * a + 32, 0:4], float(c), A.add, T.pf[32 * a:32 * a + 32, 5:6], A.is_equal, deps=[hi8, hpf])
+    tab[1] = tables(1)
     h0 = ts(T.rt[:, 13:14], ph, 64.0 if b1 == 0 else 48.0, A.mult, T.rt[:, 12:13] if b1 == 0 else p8, A.add, deps=[hp8])
     h1 = ts(T.rt[:, 14:15], ph, 4.0 if b2 == 0 else -24.0, A.mult, T.rt[:, 12:13] if b2 == 0 else p8, A.add, deps=[hp8])
-    tab[2] = tables(2, [(2, 64)])
+    tab[2] = tables(2)
     ts(T.ls[:, LY[0]:LY[0] + 6], T.ct[:, LY[0]:LY[0] + 6], T.rt[:, 13:14], A.add, deps=[h0, hcy])
     hly = ts(T.ls[:, LY[1]:LY[1] + 3], T.ct[:, LY[1]:LY[1] + 3], T.rt[:, 14:15], A.add, deps=[h1, hcy])
     outputs(0, hm0, hqw, hly, 0, 96)
@@ -377,11 +404,12 @@ def rank_program(g, core, T, topo):
     hm2, hpt = level(2, 64, 96, [(("m1", 0), ("m1", 0, 128))], [hm1], ("m1", 0, 128), [(0, 88, 0)], 88,
                      lambda: outputs(1, hm1, hqw, hly, 96, 48))
     dma("y", "o1", [hpt], T.pt[0:1, 144:168], T.ptf[64:67, 16:24])
+    hy = [mm(BY + 512 * o, ("w", 128 * o), ("m2", 0, 128), True, True, [hm2, free["y"]]) for o in range(2)]
     dma("y", "o1", [hm2], T.oc[:, 0:96], T.qm2[:, 0:24].bitcast(dt.uint8))
     for k in range(4):
-        dma("y" if k < 1 else "s", "o1" if k < 1 else "o2", [hm2], T.osc[4 * k:4 * k + 4, 0:24], T.sm2[32 * k:32 * k + 4, 0:24])
-    for o in range(2):
-        h = mm(BY + 512 * o, ("w", 128 * o), ("m2", 0, 128), True, True, [hm2, free["y"]])
-        h = cp(T.yo[:, 168 * o + 144:168 * o + 168], T.ps[:, BY + 512 * o:BY + 512 * o + 24], [h])
-        dma("y" if o == 0 else "s", "o1" if o == 0 else "o2", [h], T.y[:, 168 * o + 144:168 * o + 168], T.yo[:, 168 * o + 144:168 * o + 168])
+        dma("y" if k < 2 else "s", "o1" if k < 2 else "o2", [hm2], T.osc[4 * k:4 * k + 4, 0:24], T.sm2[32 * k:32 * k + 4, 0:24])
+    h = cp(T.yo[:, 144:168], T.ps[:, BY:BY + 24], [hy[0]])
+    dma("y", "o1", [h], T.y[:, 144:168], T.yo[:, 144:168])
+    h = act(T.yo[:, 312:336], T.ps[:, BY + 512:BY + 536], deps=[hy[1]])
+    dma("s", "o2", [h], T.y[:, 312:336], T.yo[:, 312:336])
     wait("g", [(k, count[k]) for k in ("v", "s", "p", "g", "loc", "o1", "o2")])

@@ -2,13 +2,14 @@ from concourse.bass import DstId, RemoteDMATransfer
 from concourse.mybir import dt, AluOpType, ActivationFunctionType
 
 SCRATCH = {"ps": ("psum", [128, 4096], "float32")}
-for _n, _w in dict(x=192, w=256, g=128, o=144, l0=256, l1=320, m0=256, m1=128, m2=128, e=512, u=128, d=128).items():
+for _n, _w in dict(x=192, w=256, g=96, o=144, l0=256, l1=320, m0=256, m1=128, m2=128, e=512, u=128, d=128).items():
     SCRATCH["q" + _n] = ("sbuf", [128, _w], "float8_e4m3fn_x4")
     SCRATCH["s" + _n] = ("sbuf", [128, _w], "uint8")
 for _d, _b in {"bfloat16": dict(xt=[768], wt=[1024], et=[516], ut=[512], ones=[128], ident=[128], u64=[64], dg=[816], mt=[1056],
-                                d0=[1024], d1=[800], d2=[352], am0=[512], am1=[448], am2=[96]),
+                                d0=[1024], d1=[800], d2=[352], am0=[448], am1=[352], am2=[96]),
                "int32": dict(pi=[1], pj=[8], fa=[136], fb=[136]), "uint16": dict(ls=[128], off=[96]),
-               "float32": dict(pf=[8], rt=[16], ct=[128], i8=[8], m4=[8], wd=[304], pwn=[96], pwb=[64], tt=[8, 32], ge=[40, 4], go=[48, 4],
+               "float32": dict(pf=[8], rt=[16], ct=[128], i8=[8], m4=[8], wd=[304], pwn=[48], pwb=[64], tt=[8, 32],
+                               ge=[40, 4], go=[48, 4], he=[4, 40], ho=[4, 48],
                                z=[9, 272], cs=[8, 96], cd=[8, 28], wj=[8, 8], ptf=[24], yt=[512], yo=[336])}.items():
     for _n, _w in _b.items():
         SCRATCH[_n] = ("sbuf", [128] + _w, _d)
@@ -20,8 +21,8 @@ FIRST = -2.0 ** -22
 BG, BR, BY, BD = 0, 512, 1024, 2048
 ZQ, ZK, ZO, ZP, ZA = 20, [5, 6], [(6, 31), (1, 25)], [30, 26], 6
 CQ, CK, CO = 4, [4, 3], [(3, 7), (5, 8)]
-ORDER = ("e1 S0 s0 e0 s1 S1 b1 s2 S2 a1 b2 S3 s3 a2 K1 k1 S4 s4 K2 k2 s5 b4 S5 b3-5 a3-5 a4 s6 K3 k3 a6 S6 K4 k4 s7 b6 k5 K5 "
-         "a7 b7 k6 K6 k7").split()
+ORDER = ("e1 e0 s0 S0 s1 S1 a1 s2 S2 b1 b2 s3 S3 K1 k1 a2 b3 s4 S4 a3 K2 k2 a4 s5 S5 b4 k3 K3 b5 s6 S6 a5 K4 k4 b6 s7 a6 k5 K5 "
+         "a7 b7 K6 k6 k7").split()
 
 
 def fit(vals, dims):
@@ -38,12 +39,12 @@ def fit(vals, dims):
     return [[st, n] for st, n in zip(steps, dims)], vals[0]
 
 
-def piece(kind, dims, f):
+def piece(kind, dims, f, high=0):
     idx = [[]]
     for n in dims:
         idx = [a + [k] for a in idx for k in range(n)]
     rows = [f(*a) for a in idx]
-    return {"kind": kind, "dims": dims, "key": [t[0] for t in rows], "base": [t[1] for t in rows], "src": [t[2] for t in rows]}
+    return {"kind": kind, "dims": dims, "key": [t[0] for t in rows], "base": [t[1] - high for t in rows], "src": [t[2] for t in rows], "high": high}
 
 
 def rank_program(g, core, T, topo):
@@ -113,30 +114,22 @@ def rank_program(g, core, T, topo):
         return op("p", deps, lambda: P.matmul_mx(T.ps[:, bank:bank + n], T["q" + s][:, sa:sa + 128], T["s" + s][:, sa:sa + 128],
                                                  T["q" + m][:, ma:ma + n], T["s" + m][:, ma:ma + n], start, stop))
 
+    upper, slots = [b0, b1, b2], [16, 8, 8]
+
+    def pair(L, key, blk, nat, i):
+        return (key, blk, nat + i) if upper[L] else (key, nat, blk + slots[L] * i)
+
     def at0(x, lo, a, i):
         u = (x ^ b1) + 2 * (lo ^ b2)
-        return (36 * a + u, 8 * u + 32 * a, 128 + 16 * i + u + 4 * a)
-    if b1 == 0:
-        pc0 = [piece("blk", [8, 2, 4], lambda i, lo, a, x=x: at0(x, lo, a, i)) for x in (0, 1)]
-        cB1, cB2, cA1, cA2 = 88, 0, 136, 24
-    else:
-        pc0 = [piece("nat", [2, 3, 8], lambda lo, a, i, x=x: at0(x, lo, a, i)) for x in (1, 0)]
-        cB1, cB2, cA1, cA2 = 0, 48, 72, 136
-
-    def own1(lo, m, i):
-        return (36 * lo + m, cB1 + 24 * lo + 8 * m, cA1 + 8 * i + 4 * lo + m)
-
-    def far1(m, i):
-        return (68 + m, cB2 + 8 * m, cA2 + 8 * i + 4 + m)
-    if b2 == 0:
-        pc1 = [piece("blk", [8, 2, 4], lambda i, lo, m: own1(lo, m, i)), piece("nat", [3, 8], far1)]
-    else:
-        pc1 = [piece("blk", [8, 2, 4], lambda i, h, m: far1(m, i)), piece("nat", [2, 3, 8], own1)]
-    pcs = [pc0, pc1, [piece("nat", [3, 8], lambda m, i: (64 + m, 64 + 8 * m, 8 * i + m))]]
+        return pair(0, 36 * a + u, 128 * (1 - b0) + 4 * a + u, 128 * b0 + 32 * a + 8 * u, i)
+    pcs = [[piece("nat", [2, 3, 8], lambda lo, a, i: at0(1, lo, a, i)), piece("blk", [8, 2, 4], lambda i, lo, a: at0(0, lo, a, i))],
+           [piece("blk", [8, 2, 4], lambda i, lo, m: pair(1, 36 * lo + m, 4 * lo + m, 128 + 24 * lo + 8 * m, i), 0 if b1 else 128),
+            piece("nat", [3, 8], lambda m, i: pair(1, 68 + m, 68 + m, 176 + 8 * m, i), 64 if b1 else 176)],
+           [piece("nat", [3, 8], lambda m, i: pair(2, 64 + m, m, 64 + 8 * m, i))]]
     ncol = [sum(len(p["key"]) for p in pc) for pc in pcs]
     WO = [0, 144, 272]
     MO = [544, 96, 0]
-    LG, LO, LA, LY = 0, 8, [18, 50, 78], [84, 90]
+    LG, LO, LA, LY, LT = 0, 8, [18, 50, 78], [84, 90], 96
     OO = [0, 32, 64]
 
     def terms(L, deps):
@@ -167,14 +160,8 @@ def rank_program(g, core, T, topo):
     hx = dma("y", "ldx", [], T.xt[:], T.x[:])
     hones = mset(T.ones[:], 1.0)
     hp = op("g", [], lambda: g.iota(T.pi[:], [[0, 1]], 0, 1))
-    if b0 == 0:
-        iota(T.ct[:, LG:LG + 8], [8 + i for i in range(8)], [8])
-        hct = iota(T.ct[:, LO:LO + 9], [i for i in range(9)], [9])
-        nG, nO = 128, 144
-    else:
-        iota(T.ct[:, LG:LG + 8], [32 * c for c in range(8)], [8])
-        hct = iota(T.ct[:, LO:LO + 8], [8 + 32 * c for c in range(8)], [8])
-        nG, nO = 96, 128
+    hcg = iota(T.ct[:, LG:LG + 6], [32 * c + 8 * (1 - b0) for c in range(6)], [6])
+    hco = iota(T.ct[:, LO:LO + 9], [8 * b0 + i for i in range(9)], [9])
     hid = op("g", [hones], lambda: g.affine_select(T.ident[:], T.ones[:], [[-1, 128]], A.is_equal, 0.0, 0, 1))
     hi8 = iota(T.i8[:], list(range(8)), [8])
     hu64 = op("g", [hones], lambda: g.affine_select(T.u64[:], T.ones[:, 0:64], [[1, 4], [0, 4], [-1, 4]], A.is_equal, 0.0, 0, 0))
@@ -182,22 +169,28 @@ def rank_program(g, core, T, topo):
     hdg = mset(T.dg[:], 0.0)
     for k, (sh, mk) in enumerate([(0, 15), (0, 7), (3, 1), (2, 3), (0, 3), (0, 127)]):
         hj = ts(T.pj[:, k:k + 1], T.pi[:], sh, A.logical_shift_right, mk, A.bitwise_and, deps=[hp])
-    mset(T.ge[:, 0:40:5, :], 0.0)
-    mset(T.go[:, 0:48:6, :], 0.0)
+    fills = [(T.cd[:, 2:8:2, 2:28:4], 0.0), (T.cs[:, 1:8, CQ:CQ + 1], FIRST), (T.cs[:, 0, CQ:CQ + 84:12], FIRST), (T.cs[:, 0, CQ + 8:CQ + 84:12], FIRST),
+             (T.cs[:, 0:8:2, CQ + 4:CQ + 84:12], 8.0), (T.mt[:, 992:1056], 0.0)]
+    if 0 in upper:
+        fills += [(T.ge[:, 0:40:5, :], 0.0), (T.go[:, 0:48:6, :], 0.0), (T.go[:, 1:48:6, :], 0.0)]
+    if 1 in upper:
+        fills += [(T.he[:, :, 0:40:5], 0.0), (T.ho[:, :, 0:48:6], 0.0), (T.ho[:, :, 1:48:6], 0.0)]
+
+    def fill(n):
+        for _ in range(min(n, len(fills))):
+            mset(*fills.pop())
+    fill(2)
     hpf = cp(T.pf[:, 0:6], T.pj[:, 0:6], [hj])
     p16, p8, ph, p4, pq, pp = [T.pf[:, k:k + 1] for k in range(6)]
-    mset(T.go[:, 1:48:6, :], 0.0)
-    mset(T.cd[:, 2:8:2, 2:28:4], 0.0)
-    if b0 == 0:
-        h = ts(T.rt[:, 0:1], p16, 11.0, A.min, 16.0, A.mult, deps=[hpf])
-    else:
-        h = ts(T.rt[:, 0:1], ph, 16.0, A.mult, p8, A.add, deps=[hpf])
-    mset(T.cs[:, 1:8, CQ:CQ + 1], FIRST)
-    mset(T.cs[:, 0, CQ:CQ + 84:12], FIRST)
-    hl = ts(T.ls[:, 0:LO + nO // 16], T.ct[:, 0:LO + nO // 16], T.rt[:, 0:1], A.add, 191.0, A.min, deps=[h, hct])
+    fill(2)
+    h = ts(T.rt[:, 0:1], ph, 16.0, A.mult, p8, A.add, deps=[hpf])
+    h2 = ts(T.rt[:, 15:16], p16, 11.0, A.min, 16.0, A.mult, deps=[hpf])
+    fill(1)
+    hlg = ts(T.ls[:, LG:LG + 6], T.ct[:, LG:LG + 6], T.rt[:, 0:1], A.add, deps=[h, hcg])
+    hlo = ts(T.ls[:, LO:LO + 9], T.ct[:, LO:LO + 9], T.rt[:, 15:16], A.add, 191.0, A.min, deps=[h2, hco])
 
     for i in range(8):
-        hpw = act(T.pwn[:, i:96:8], T.ones[:, 0:12], -8.0 ** (8 - i) if i else 0.0, deps=[hones])
+        hpw = act(T.pwn[:, i:48:8], T.ones[:, 0:6], -8.0 ** (8 - i) if i else 0.0, deps=[hones])
     for i in range(8):
         hpb = act(T.pwb[:, 8 * i:8 * i + 8], T.ones[:, 0:8], -8.0 ** (8 - i) if i else 0.0)
     for e in range(4):
@@ -208,11 +201,11 @@ def rank_program(g, core, T, topo):
 
     hqx = quant("x", 0, 192, T.xt[:], [hx])
 
-    def pick(b, n, lst, scales):
+    def pick(b, n, lst, hl, scales):
         o = T.ls[:, lst:lst + n // 16]
         hc = cp(T["q" + b][:, 0:n].bitcast(dt.uint32), T.qx[:, 0:192].bitcast(dt.uint32).indirect(o), [hqx, hl])
         return hc, scales(T["s" + b][:, 0:n], T.sx[:, 0:192].indirect(o), [hqx, hl])
-    hgc, hgs = pick("g", nG, LG, cp)
+    hgc, hgs = pick("g", 96, LG, hlg, cp)
 
     def bits(es):
         return sum(1 << e for e in es)
@@ -220,30 +213,37 @@ def rank_program(g, core, T, topo):
     rid, pid = topo.addr(mate, core)
     es = topo.engines(core, mate)
     wait("g", [hgc])
-    g.remote_dma(T.ql0[:, 0:nG].bitcast(dt.uint8), T.qg[:, 0:nG].bitcast(dt.uint8), T.sem.a1, T.sem.loc, pid, rid, bits(es))
+    g.remote_dma(T.ql0[:, 0:96].bitcast(dt.uint8), T.qg[:].bitcast(dt.uint8), T.sem.a1, T.sem.loc, pid, rid, bits(es))
     wait("g", [hgs])
-    g.remote_dma(T.sl0[:, 0:nG], T.sg[:, 0:nG], T.sem.a1, T.sem.loc, pid, rid, bits(es))
+    g.remote_dma(T.sl0[:, 0:96], T.sg[:], T.sem.a1, T.sem.loc, pid, rid, bits(es))
     count["loc"] += 2 * len(es)
     ha1 = ("a1", 2 * len(topo.engines(mate, core)))
     hw = dma("y", "ldw", [ha1], T.wt[:], T.w[:])
-    hwd = [weights(0, [hpw, hpb])]
-    hb = [bases(0, [hdg, hwd[0]])]
-    hb.append(bases(1, []))
-    hb.append(bases(2, []))
-    hterm += [terms(1, [hb[2]]), terms(2, [])]
-    hwd += [weights(1, []), weights(2, [])]
-    iota(T.ct[:, LY[0]:LY[0] + 6], [(4 * (c ^ b2) + a) if b1 == 0 else (24 * (c ^ b2) + 8 * a) for a in range(3) for c in range(2)], [3, 2])
-    hcy = iota(T.ct[:, LY[1]:LY[1] + 3], [m if b2 == 0 else 88 + 8 * m for m in range(3)], [3])
 
-    hoc, hos = pick("o", nO, LO, gat)
+    hoc, hos = pick("o", 144, LO, hlo, gat)
+    v, hh = WO[1], hdg
+    for p in pcs[1]:
+        if p["high"]:
+            hh = mset(T.dg[96:98, v:v + len(p["key"])], float(p["high"]), [hdg])
+        v += len(p["key"])
+    hwd = [weights(0, [hpw, hpb])]
+    bases(0, [hh, hwd[0]])
+    bases(1, [])
+    hb = bases(2, [])
+    hterm += [terms(1, [hb]), terms(2, [])]
+    hwd += [weights(1, []), weights(2, [])]
+    ycol = [[(24 * (c ^ b2) + 8 * a) if k ^ b1 else (48 + 4 * (c ^ b2) + a) for a in range(3) for c in range(2)] for k in range(2)]
+    iota(T.ct[:, LY[0]:LY[0] + 6], ycol[0], [3, 2])
+    iota(T.ct[:, LT:LT + 6], [y1 - y0 for y0, y1 in zip(*ycol)], [3, 2])
+    hcy = iota(T.ct[:, LY[1]:LY[1] + 3], [m + 4 * b2 for m in range(3)], [3])
+
     for b in range(4):
         hqe = quant("e", 128 * b, 128, T.et[:, 3 - b:515 - b], [he])
-    hz = quant("l0", 96 if b0 == 0 else 128, 128, T.dg[:, 304:816], [hdg])
+    hz = quant("l0", 96, 128, T.dg[:, 304:816], [hdg])
     h = mset(T.z[:, 0:8:2, ZQ:ZQ + 240:6], LOW)
     mset(T.z[:, 1:8:2, ZQ:ZQ + 240:5], LOW)
     mset(T.cs[:, 1:8:2, CQ + 3:CQ + 84:3], 8.0)
-    mset(T.cs[:, 0:8:2, CQ + 4:CQ + 84:12], 8.0)
-    mset(T.cs[:, 0, CQ + 8:CQ + 84:12], FIRST)
+    fill(16)
     mset(T.z[:, 0, ZQ + 6:ZQ + 7], 0.0, [h])
     cp(T.cd[:, 1:8:2, 1:21:3], T.wj[:, 1:8:2, 1:8], [hwj])
     cp(T.cd[:, 2:8:2, 1:28:4], T.wj[:, 2:8:2, 1:8], [hwj])
@@ -262,7 +262,7 @@ def rank_program(g, core, T, topo):
         return h
     for k in range(8):
         hut = act(T.ut[:, 64 * k:64 * k + 64], T.u64[:], 4.0, deps=[hu64])
-    decode_cp(decode_mm(("o", 0, 128), [hoc, hos]), "d0", [(0, 128, 128 if b0 == 0 else 0)])
+    decode_cp(decode_mm(("o", 0, 128), [hoc, hos]), "d0", [(0, 128, 128 * (1 - b0))])
     for L in range(3):
         hw8 = act(T.wd[:, WO[L] + ncol[L]:WO[L] + ncol[L] + 8], T.pwn[:, 0:8], deps=[hpw])
     rts = {}
@@ -280,26 +280,28 @@ def rank_program(g, core, T, topo):
             c += m
         return hla
     tab = [tables(0), None, None]
-    if b1 == 1:
-        mset(T.mt[:, 928:1056], 0.0)
-        quant("m0", 128, 128, T.dg[:, 304:816], [hdg])
     hqu = quant("u", 0, 128, T.ut[:], [hut])
 
     def level(L, lo, hi, prods, deps, dec, runs, dcols, mid=None):
-        n, v = ncol[L], WO[L]
+        n, v, up = ncol[L], WO[L], upper[L]
+        step = float(slots[L] if up else 1)
         dw, am = T["d%d" % L][:, 0:4 * dcols], T["am%d" % L][:, 0:4 * n]
         for k, (st, mv) in enumerate(prods):
             hg = mm(BG, st, mv, k == 0, k == len(prods) - 1, deps)
         hs = decode_mm(dec, deps)
-        nt = 2 if L == 0 else 4
-        for k in range(nt):
-            ht = op("v", [hg], lambda: V.transpose(T.tt[lo:hi, k:8:nt, :], T.ps[lo:hi, BG + 32 // nt * k:BG + 32 // nt * k + 256 // nt]))
-        gs = [T.ge, T.go]
+        nt = 32 // slots[L]
+        ht = {}
+        for k in list(range(0, nt, 2)) + list(range(1, nt, 2)):
+            ht[k % 2] = op("v", [hg], lambda: V.transpose(T.tt[lo:hi, k:8:nt, :], T.ps[lo:hi, BG + 32 // nt * k:BG + 32 // nt * k + 256 // nt]))
 
         def mask(f, par, s):
-            c = 4 * (L % 2) + s
-            o, i, m = gs[par][lo:hi, 1 + par + s:8 * ZK[par]:ZK[par], :], T.tt[lo:hi, :, 8 * s + par:8 * s + 8:2], T.m4[lo:hi, c:c + 1]
-            return act(o, i, m, deps=[ht]) if f == "s" else ts(o, i, m, A.mult, deps=[ht])
+            c, k = 4 * (L % 2) + s, ZK[par]
+            if up:
+                o, i, d = [T.he, T.ho][par][lo:hi, :, 1 + par + s:8 * k:k], T.tt[lo:hi, par:8:2, 8 * s:8 * s + 8], ht[par]
+            else:
+                o, i, d = [T.ge, T.go][par][lo:hi, 1 + par + s:8 * k:k, :], T.tt[lo:hi, :, 8 * s + par:8 * s + 8:2], ht[1]
+            m = T.m4[lo:hi, c:c + 1]
+            return act(o, i, m, deps=[d]) if f == "s" else ts(o, i, m, A.mult, deps=[d])
         ready = [[mask("s", 0, s) for s in (2, 3)] + [mask("v", 0, s) for s in (0, 1)], [mask("s", 1, s) for s in (2, 3)]]
         hd = decode_cp(hs, "d%d" % L, runs)
         ham = gat(am, dw.indirect(T.ls[:, LA[L]:LA[L] + n // 4]), [hd, tab[L]])
@@ -308,13 +310,14 @@ def rank_program(g, core, T, topo):
         z, cs, cd = T.z, T.cs, T.cd
         done = {}
         for tok in ORDER:
-            k, j, e = tok[0], int(tok[1:].split("-")[0]), int(tok[1:].split("-")[-1])
+            k, j = tok[0], int(tok[1:])
             par = j % 2
             if k == "e":
                 ready[1].append(mask("v", 1, j))
             elif k in "sS":
                 o, st = ZO[par][k == "S"], 30 // ZK[par]
-                done[k, j] = scan(z[lo:hi, j + 1, o:o + 240:st], z[lo:hi, j, ZQ:ZQ + 240:st], gs[par][lo:hi, :, j // 2], LOW, A.max, A.add,
+                gs = [T.he, T.ho][par][lo:hi, j // 2, :] if up else [T.ge, T.go][par][lo:hi, :, j // 2]
+                done[k, j] = scan(z[lo:hi, j + 1, o:o + 240:st], z[lo:hi, j, ZQ:ZQ + 240:st], gs, LOW, A.max, A.add,
                                   [done.get(("s", j - 1)), done.get(("S", j - 1))] + ready[par])
             elif k in "kK":
                 o, st = CO[par][k == "K"], 12 // CK[par]
@@ -323,20 +326,16 @@ def rank_program(g, core, T, topo):
             else:
                 c, was, now = CK[par], ZP[1 - par], ZP[par]
                 if k == "a":
-                    hc = tt(cd[lo:hi, j:e + 1:2, 0:7 * c:c], z[lo:hi, j:e + 1:2, was:was + 210:30], z[lo:hi, j + 1:e + 2:2, now:now + 210:30],
-                            A.is_ge, deps=[done["s", e]])
+                    done[k, j] = tt(cd[lo:hi, j, 0:7 * c:c], z[lo:hi, j, was:was + 210:30], z[lo:hi, j + 1, now:now + 210:30], A.is_ge, deps=[done["s", j]])
                 else:
-                    hc = tt(cd[lo:hi, j:e + 1:2, c - 1:7 * c:c], z[lo:hi, j:e + 1:2, was + 30:was + 240:30], z[lo:hi, j + 1:e + 2:2, ZA + 30:ZA + 240:30],
-                            A.is_gt, deps=[done["s", e]])
-                for col in range(j, e + 1, 2):
-                    done[k, col] = hc
+                    done[k, j] = tt(cd[lo:hi, j, c - 1:7 * c:c], z[lo:hi, j, was + 30:was + 240:30], z[lo:hi, j + 1, ZA + 30:ZA + 240:30], A.is_gt, deps=[done["s", j]])
         last = CO[1][0] + 80
         cuts = [(0, n + 8)] if n < 64 else [(0, n // 2), (n // 2, n + 8)]
         h = [ts(T.fa[lo:hi, a:b], T.wd[lo:hi, v + a:v + b], cs[lo:hi, 7, last:last + 1], A.mult, -0.5, A.add, deps=[done["k", 7], hwd[L], hw8]) for a, b in cuts]
         h = [ts(T.fb[lo:hi, a:b], T.fa[lo:hi, a:b], 7, A.bitwise_and, deps=[d]) for (a, b), d in zip(cuts, h)]
-        hdig = [cp(T.dg[lo:hi, v + a:v + b], T.fb[lo:hi, a:b], [d]) for (a, b), d in zip(cuts, h)][-1]
-        h = quant("d", 0, 128, T.dg[:, v:v + 512], [hdig, hb[2]])
-        hpt = act(T.ptf[lo:hi, 8 * L:8 * L + 8], T.dg[lo:hi, v + n:v + n + 8], deps=[hdig])
+        hdig = [ts(T.dg[lo:hi, v + a:v + b], T.fb[lo:hi, a:b], step, A.mult, deps=[d]) for (a, b), d in zip(cuts, h)][-1]
+        h = quant("d", 0, 128, T.dg[:, v:v + 512], [hdig, hb])
+        hpt = act(T.ptf[lo:hi, 8 * L:8 * L + 8], T.dg[lo:hi, v + n:v + n + 8], 1.0 / step, deps=[hdig])
         h = mm(BR, ("u", 0), ("d", 0, 128), True, True, [h, hqu])
         o = T.off[:, OO[L]:OO[L] + n // 4]
         h = ts(o, T.ps[:, BR:BR + n // 4], pq, A.add, deps=[h])
@@ -352,10 +351,9 @@ def rank_program(g, core, T, topo):
             h = gat(T.yo[:, y0:y0 + n], T.yt[:, w0:w0 + 128].indirect(T.ls[:, LY[L]:LY[L] + n // 16]), [hc[o], hly])
             dma("y", "o1", [h, ha2], T.y[:, y0:y0 + n], T.yo[:, y0:y0 + n])
 
-    prods = [(("l0", 0), ("o", 0, 144))] if b0 == 0 else [(("o", 0), ("l0", 0, 144))]
-    hm0, hpt = level(0, 0, 96, prods, [ha1, hz, hoc, hos], ("l0", 0, 128), [(0, 128, 128 * b0)], 256)
+    hm0, hpt = level(0, 0, 96, [(("l0", 0), ("o", 0, 144))], [ha1, hz, hoc, hos], ("l0", 0, 128), [(0, 128, 128 * b0)], 256)
 
-    plan = [(2, 64, 0), (6, 64, 64), (4, 0, 0)] if b1 == 0 else [(2, 0, 64), (6, 24, 256), (4, 72, 256)]
+    plan = [(2, 0, 64), (6, 24, 256), (4, 48, 0)]
     es = [e for e in topo.engines(core, T.cores[r ^ 2]) if all(e in topo.engines(core, T.cores[r ^ x]) for x in (4, 6))]
     k4 = len(es) // 4
     sets = [[es[0:k4], es[k4:2 * k4], es[2 * k4:4 * k4]], [es[2 * k4:3 * k4], es[3 * k4:4 * k4], es[0:2 * k4]]]
@@ -375,27 +373,27 @@ def rank_program(g, core, T, topo):
     for a in range(3):
         dma("y", "o1", [hpt, ha2], T.pt[0:1, 32 * a:32 * a + 32], T.ptf[36 * a:36 * a + 4, 0:8])
 
-    decode_cp(decode_mm(("m0", 0, 128), [hm0]), "d1", [(0, 64, cA1)] if b1 == 0 else [(48, 48, cB1)])
+    decode_cp(decode_mm(("m0", 0, 128), [hm0]), "d1", [(48, 64, 0)])
     hqw = quant("w", 0, 256, T.wt[:], [hw])
+    quant("m0", 128, 128, T.dg[:, 304:816], [hdg])
     hz1 = quant("l1", 128, 128, T.dg[:, 304:816], [hdg])
     hp8 = ts(T.rt[:, 12:13], p8, 8.0, A.mult, deps=[hpf])
-    if b2 == 0:
-        mset(T.mt[:, 448:544], 0.0)
+    h0 = ts(T.rt[:, 13:14], ph, 7.0 if b1 else -7.0, A.mult, 1.0 if b1 else 8.0, A.add, deps=[hpf])
+    mset(T.mt[:, 448:544], 0.0)
     for a, c in [(0, -1), (1, 36), (2, 67)]:
         ts(T.m4[32 * a:32 * a + 32, 4:8], T.i8[32 * a:32 * a + 32, 0:4], float(c), A.add, T.pf[32 * a:32 * a + 32, 5:6], A.is_equal, deps=[hi8, hpf])
+    h0 = ts(T.rt[:, 11:12], T.rt[:, 13:14], p8, A.mult, deps=[h0])
+    h1 = ts(T.rt[:, 14:15], ph, -4.0 if b2 else 4.0, A.mult, T.rt[:, 12:13], A.add, deps=[hp8])
     tab[1] = tables(1)
-    h0 = ts(T.rt[:, 13:14], ph, 64.0 if b1 == 0 else 48.0, A.mult, T.rt[:, 12:13] if b1 == 0 else p8, A.add, deps=[hp8])
-    h1 = ts(T.rt[:, 14:15], ph, 4.0 if b2 == 0 else -24.0, A.mult, T.rt[:, 12:13] if b2 == 0 else p8, A.add, deps=[hp8])
+    h0 = ts(T.ct[:, LT + 8:LT + 14], T.ct[:, LT:LT + 6], ph, A.mult, T.rt[:, 11:12], A.add, deps=[h0, hcy])
     tab[2] = tables(2)
-    ts(T.ls[:, LY[0]:LY[0] + 6], T.ct[:, LY[0]:LY[0] + 6], T.rt[:, 13:14], A.add, deps=[h0, hcy])
-    hly = ts(T.ls[:, LY[1]:LY[1] + 3], T.ct[:, LY[1]:LY[1] + 3], T.rt[:, 14:15], A.add, deps=[h1, hcy])
+    h0 = tt(T.ct[:, LT + 16:LT + 22], T.ct[:, LT + 8:LT + 14], T.ct[:, LY[0]:LY[0] + 6], A.add, deps=[h0])
+    ts(T.ls[:, LY[1]:LY[1] + 3], T.ct[:, LY[1]:LY[1] + 3], T.rt[:, 14:15], A.add, deps=[h1, hcy])
+    hly = cp(T.ls[:, LY[0]:LY[0] + 6], T.ct[:, LT + 16:LT + 22], [h0])
     outputs(0, hm0, hqw, hly, 0, 96)
 
-    if b1 == 0:
-        prods, runs = [(("l1", 56), ("m0", 0, 128)), (("l1", 184), ("l1", 0, 128))], [(256, 24, cB2), (0, 112, cA2)]
-    else:
-        prods, runs = [(("m0", 40), ("l1", 0, 128)), (("l1", 184), ("l1", 64, 128))], [(256, 24, cB2), (0, 128, cA1)]
-    hm1, hpt = level(1, 0, 96, prods, [ha2, hz1, hm0], ("l1", 0, 280), runs, 200)
+    hm1, hpt = level(1, 0, 96, [(("l1", 56), ("m0", 48, 128)), (("l1", 184), ("l1", 0, 128))], [ha2, hz1, hm0], ("l1", 0, 280),
+                     [(256, 24, 176), (0, 112, 64)], 200)
     for lo in range(2):
         for m in range(3):
             k = (lo ^ b2) + 2 * m

@@ -2,15 +2,15 @@ from concourse.bass import DstId, RemoteDMATransfer
 from concourse.mybir import dt, AluOpType, ActivationFunctionType
 
 SCRATCH = {"ps": ("psum", [128, 4096], "float32")}
-for _n, _w in dict(x=192, w=256, g=96, o=144, l0=256, l1=320, m0=256, m1=128, m2=128, e=512, u=128, d=128).items():
+for _n, _w in dict(w=256, g=128, l0=240, l1=320, m0=256, m1=128, m2=32, e=512, u=128, v=132, d=132, a=192, b=192, c=192).items():
     SCRATCH["q" + _n] = ("sbuf", [128, _w], "float8_e4m3fn_x4")
     SCRATCH["s" + _n] = ("sbuf", [128, _w], "uint8")
-for _d, _b in {"bfloat16": dict(xt=[768], wt=[1024], et=[516], ut=[512], ones=[128], ident=[128], u64=[64], dg=[816], mt=[1056],
-                                d0=[1024], d1=[800], d2=[352], am0=[448], am1=[352], am2=[96]),
+for _d, _b in {"bfloat16": dict(xt=[24, 8, 4], xo=[1088], wt=[1024], et=[516], ut=[512], vt=[528], ones=[128], ident=[128], u64=[64], v32=[32],
+                                dg=[816], mt=[1536], d0=[1024], d1=[800], am0=[448], am1=[352], pairs=[768]),
                "int32": dict(pi=[1], pj=[8], fa=[136], fb=[136]), "uint16": dict(ls=[128], off=[96]),
-               "float32": dict(pf=[8], rt=[16], ct=[128], i8=[8], m4=[8], wd=[304], pwn=[48], pwb=[64], tt=[8, 32],
+               "float32": dict(pf=[8], rt=[16], ct=[160], i8=[8], m4=[8], wd=[304], pwn=[48], pwb=[64], tt=[8, 32],
                                ge=[40, 4], go=[48, 4], he=[4, 40], ho=[4, 48],
-                               z=[9, 272], cs=[8, 96], cd=[8, 28], wj=[8, 8], ptf=[24], yt=[512], yo=[336])}.items():
+                               z=[9, 272], cs=[8, 96], cd=[8, 28], wj=[8, 8], ptf=[24], yt=[640], yo=[336], yp=[384], yz=[64])}.items():
     for _n, _w in _b.items():
         SCRATCH[_n] = ("sbuf", [128] + _w, _d)
 SEMAPHORES = ["v", "s", "p", "g", "ldx", "ldw", "a1", "a2", "loc", "o1", "o2"]
@@ -21,8 +21,8 @@ FIRST = -2.0 ** -22
 BG, BR, BY, BD = 0, 512, 1024, 2048
 ZQ, ZK, ZO, ZP, ZA = 20, [5, 6], [(6, 31), (1, 25)], [30, 26], 6
 CQ, CK, CO = 4, [4, 3], [(3, 7), (5, 8)]
-ORDER = ("e1 e0 s0 S0 s1 S1 a1 s2 S2 b1 b2 s3 S3 K1 k1 a2 b3 s4 S4 a3 K2 k2 a4 s5 S5 b4 k3 K3 b5 s6 S6 a5 K4 k4 b6 s7 a6 k5 K5 "
-         "a7 b7 K6 k6 k7").split()
+ORDER = ("e1 e0 s0 S0 f0 s1 S1 f0 d0 a1 s2 S2 b1 b2 s3 S3 K1 k1 a2 b3 s4 S4 a3 K2 k2 a4 s5 S5 b4 k3 K3 b5 s6 S6 a5 K4 k4 b6 s7 a6 k5 K5 "
+         "a7 b7 K6 k6 f0 k7").split()
 
 
 def fit(vals, dims):
@@ -83,6 +83,9 @@ def rank_program(g, core, T, topo):
         pat, base = fit(vals, dims)
         return op("g", deps, lambda: g.iota(out, pat, base, 0, allow_small_or_imprecise_dtypes=True))
 
+    def select(out, in_, pat, how, base, step, deps):
+        return op("g", deps, lambda: g.affine_select(out, in_, pat, how, 0.0, base, step))
+
     def mset(ap, c, deps=()):
         return op("v", deps, lambda: V.memset(ap, c))
 
@@ -114,6 +117,13 @@ def rank_program(g, core, T, topo):
         return op("p", deps, lambda: P.matmul_mx(T.ps[:, bank:bank + n], T["q" + s][:, sa:sa + 128], T["s" + s][:, sa:sa + 128],
                                                  T["q" + m][:, ma:ma + n], T["s" + m][:, ma:ma + n], start, stop))
 
+    def codes(dst, a, src, width, o, deps):
+        n = 16 * o.shape[1]
+        return cp(T["q" + dst][:, a:a + n].bitcast(dt.uint32), T["q" + src][:, 0:width].bitcast(dt.uint32).indirect(o), deps)
+
+    def scales(dst, a, src, width, o, deps):
+        return gat(T["s" + dst][:, a:a + 16 * o.shape[1]], T["s" + src][:, 0:width].indirect(o), deps)
+
     upper, slots = [b0, b1, b2], [16, 8, 8]
 
     def pair(L, key, blk, nat, i):
@@ -124,12 +134,10 @@ def rank_program(g, core, T, topo):
         return pair(0, 36 * a + u, 128 * (1 - b0) + 4 * a + u, 128 * b0 + 32 * a + 8 * u, i)
     pcs = [[piece("nat", [2, 3, 8], lambda lo, a, i: at0(1, lo, a, i)), piece("blk", [8, 2, 4], lambda i, lo, a: at0(0, lo, a, i))],
            [piece("blk", [8, 2, 4], lambda i, lo, m: pair(1, 36 * lo + m, 4 * lo + m, 128 + 24 * lo + 8 * m, i), 0 if b1 else 128),
-            piece("nat", [3, 8], lambda m, i: pair(1, 68 + m, 68 + m, 176 + 8 * m, i), 64 if b1 else 176)],
-           [piece("nat", [3, 8], lambda m, i: pair(2, 64 + m, m, 64 + 8 * m, i))]]
-    ncol = [sum(len(p["key"]) for p in pc) for pc in pcs]
+            piece("nat", [3, 8], lambda m, i: pair(1, 68 + m, 68 + m, 176 + 8 * m, i), 64 if b1 else 176)]]
+    ncol = [sum(len(p["key"]) for p in pc) for pc in pcs] + [16]
     WO = [0, 144, 272]
-    MO = [544, 96, 0]
-    LG, LO, LA, LY, LT = 0, 8, [18, 50, 78], [84, 90], 96
+    LA, LY, LP, LT, CP = [18, 50], [84, 90], 96, 96, 128
     OO = [0, 32, 64]
 
     def terms(L, deps):
@@ -145,8 +153,7 @@ def rank_program(g, core, T, topo):
         for p in pcs[L]:
             n = len(p["key"])
             pat, base = fit(p["key"], p["dims"])
-            src = T.pwb[:, 0:n] if p["kind"] == "blk" else T.pwn[:, 0:n]
-            hk = op("g", deps, lambda: g.affine_select(T.wd[:, v:v + n], src, pat, A.is_equal, 0.0, base, -1))
+            hk = select(T.wd[:, v:v + n], T.pwb[:, 0:n] if p["kind"] == "blk" else T.pwn[:, 0:n], pat, A.is_equal, base, -1, deps)
             v += n
         return hk
 
@@ -157,97 +164,86 @@ def rank_program(g, core, T, topo):
             v += len(p["key"])
         return hk
 
+    def gfill(up):
+        if up:
+            return [(T.he[:, :, 0:40:5], 0.0), (T.ho[:, :, 0:48:6], 0.0), (T.ho[:, :, 1:48:6], 0.0)]
+        return [(T.ge[:, 0:40:5, :], 0.0), (T.go[:, 0:48:6, :], 0.0), (T.go[:, 1:48:6, :], 0.0)]
+
     hx = dma("y", "ldx", [], T.xt[:], T.x[:])
     hones = mset(T.ones[:], 1.0)
     hp = op("g", [], lambda: g.iota(T.pi[:], [[0, 1]], 0, 1))
-    hcg = iota(T.ct[:, LG:LG + 6], [32 * c + 8 * (1 - b0) for c in range(6)], [6])
-    hco = iota(T.ct[:, LO:LO + 9], [8 * b0 + i for i in range(9)], [9])
-    hid = op("g", [hones], lambda: g.affine_select(T.ident[:], T.ones[:], [[-1, 128]], A.is_equal, 0.0, 0, 1))
     hi8 = iota(T.i8[:], list(range(8)), [8])
-    hu64 = op("g", [hones], lambda: g.affine_select(T.u64[:], T.ones[:, 0:64], [[1, 4], [0, 4], [-1, 4]], A.is_equal, 0.0, 0, 0))
+    hid = select(T.ident[:], T.ones[:], [[-1, 128]], A.is_equal, 0, 1, [hones])
+    hu64 = select(T.u64[:], T.ones[:, 0:64], [[1, 4], [0, 4], [-1, 4]], A.is_equal, 0, 0, [])
     hterm = [terms(0, [])]
+    hxo = mset(T.xo[:, 384:1088], 0.0)
     hdg = mset(T.dg[:], 0.0)
-    for k, (sh, mk) in enumerate([(0, 15), (0, 7), (3, 1), (2, 3), (0, 3), (0, 127)]):
-        hj = ts(T.pj[:, k:k + 1], T.pi[:], sh, A.logical_shift_right, mk, A.bitwise_and, deps=[hp])
-    fills = [(T.cd[:, 2:8:2, 2:28:4], 0.0), (T.cs[:, 1:8, CQ:CQ + 1], FIRST), (T.cs[:, 0, CQ:CQ + 84:12], FIRST), (T.cs[:, 0, CQ + 8:CQ + 84:12], FIRST),
-             (T.cs[:, 0:8:2, CQ + 4:CQ + 84:12], 8.0), (T.mt[:, 992:1056], 0.0)]
-    if 0 in upper:
-        fills += [(T.ge[:, 0:40:5, :], 0.0), (T.go[:, 0:48:6, :], 0.0), (T.go[:, 1:48:6, :], 0.0)]
-    if 1 in upper:
-        fills += [(T.he[:, :, 0:40:5], 0.0), (T.ho[:, :, 0:48:6], 0.0), (T.ho[:, :, 1:48:6], 0.0)]
 
-    def fill(n):
-        for _ in range(min(n, len(fills))):
-            mset(*fills.pop())
-    fill(2)
-    hpf = cp(T.pf[:, 0:6], T.pj[:, 0:6], [hj])
-    p16, p8, ph, p4, pq, pp = [T.pf[:, k:k + 1] for k in range(6)]
-    fill(2)
-    h = ts(T.rt[:, 0:1], ph, 16.0, A.mult, p8, A.add, deps=[hpf])
-    h2 = ts(T.rt[:, 15:16], p16, 11.0, A.min, 16.0, A.mult, deps=[hpf])
-    fill(1)
-    hlg = ts(T.ls[:, LG:LG + 6], T.ct[:, LG:LG + 6], T.rt[:, 0:1], A.add, deps=[h, hcg])
-    hlo = ts(T.ls[:, LO:LO + 9], T.ct[:, LO:LO + 9], T.rt[:, 15:16], A.add, 191.0, A.min, deps=[h2, hco])
+    def part(k, sh, mk):
+        return ts(T.pj[:, k:k + 1], T.pi[:], sh, A.logical_shift_right, mk, A.bitwise_and, deps=[hp])
+    part(0, 2, 3)
+    hj = part(1, 0, 3)
+    p4, pq, p8, ph, pp, odd = [T.pf[:, k:k + 1] for k in range(6)]
+    for f in gfill(b0):
+        mset(*f)
 
     for i in range(8):
         hpw = act(T.pwn[:, i:48:8], T.ones[:, 0:6], -8.0 ** (8 - i) if i else 0.0, deps=[hones])
-    for i in range(8):
-        hpb = act(T.pwb[:, 8 * i:8 * i + 8], T.ones[:, 0:8], -8.0 ** (8 - i) if i else 0.0)
     for e in range(4):
         act(T.et[:, e:512:4], T.ident[:], 1.0 if e == 3 else 0.0, deps=[hid])
     he = act(T.et[:, 512:516], T.ones[:, 0:4], 0.0)
+    for i in range(8):
+        hown = act(T.xo[:, 512 + 64 * i:560 + 64 * i], T.xt[:, b0:24:2, i, :], deps=[hx, hxo])
+    for i in range(8):
+        hpb = act(T.pwb[:, 8 * i:8 * i + 8], T.ones[:, 0:8], -8.0 ** (8 - i) if i else 0.0)
     for i in range(1, 8):
         hwj = act(T.wj[:, :, i], T.i8[:], -8.0 ** (i - 8), deps=[hi8])
 
-    hqx = quant("x", 0, 192, T.xt[:], [hx])
-
-    def pick(b, n, lst, hl, scales):
-        o = T.ls[:, lst:lst + n // 16]
-        hc = cp(T["q" + b][:, 0:n].bitcast(dt.uint32), T.qx[:, 0:192].bitcast(dt.uint32).indirect(o), [hqx, hl])
-        return hc, scales(T["s" + b][:, 0:n], T.sx[:, 0:192].indirect(o), [hqx, hl])
-    hgc, hgs = pick("g", 96, LG, hlg, cp)
+    h = cp(T.xo[:, 0:384], T.xt[:, 1 - b0:24:2, :, :], [hx])
+    hpf = cp(T.pf[:, 0:2], T.pj[:, 0:2], [hj])
+    v, hh = WO[1], hdg
+    for p in pcs[1]:
+        if p["high"]:
+            hh = mset(T.dg[96:98, v:v + len(p["key"])], float(p["high"]), [hdg])
+        v += len(p["key"])
+    hg0 = quant("g", 0, 128, T.xo[:, 0:512], [h, hxo])
 
     def bits(es):
         return sum(1 << e for e in es)
     mate = T.cores[r ^ 1]
     rid, pid = topo.addr(mate, core)
     es = topo.engines(core, mate)
-    wait("g", [hgc])
-    g.remote_dma(T.ql0[:, 0:96].bitcast(dt.uint8), T.qg[:].bitcast(dt.uint8), T.sem.a1, T.sem.loc, pid, rid, bits(es))
-    wait("g", [hgs])
-    g.remote_dma(T.sl0[:, 0:96], T.sg[:], T.sem.a1, T.sem.loc, pid, rid, bits(es))
+    wait("g", [hg0])
+    g.remote_dma(T.ql0[:, 0:96].bitcast(dt.uint8), T.qg[:, 0:96].bitcast(dt.uint8), T.sem.a1, T.sem.loc, pid, rid, bits(es))
+    g.remote_dma(T.sl0[:, 0:96], T.sg[:, 0:96], T.sem.a1, T.sem.loc, pid, rid, bits(es))
     count["loc"] += 2 * len(es)
     ha1 = ("a1", 2 * len(topo.engines(mate, core)))
     hw = dma("y", "ldw", [ha1], T.wt[:], T.w[:])
 
-    hoc, hos = pick("o", 144, LO, hlo, gat)
-    v, hh = WO[1], hdg
-    for p in pcs[1]:
-        if p["high"]:
-            hh = mset(T.dg[96:98, v:v + len(p["key"])], float(p["high"]), [hdg])
-        v += len(p["key"])
     hwd = [weights(0, [hpw, hpb])]
     bases(0, [hh, hwd[0]])
-    bases(1, [])
-    hb = bases(2, [])
-    hterm += [terms(1, [hb]), terms(2, [])]
-    hwd += [weights(1, []), weights(2, [])]
-    ycol = [[(24 * (c ^ b2) + 8 * a) if k ^ b1 else (48 + 4 * (c ^ b2) + a) for a in range(3) for c in range(2)] for k in range(2)]
+    hb = bases(1, [])
+    hterm.append(terms(1, [hb]))
+    hwd.append(weights(1, []))
+    ycol = [[(24 * (c ^ b2) + 8 * a) if k ^ b1 else (128 + 4 * (c ^ b2) + a) for a in range(3) for c in range(2)] for k in range(2)]
     iota(T.ct[:, LY[0]:LY[0] + 6], ycol[0], [3, 2])
     iota(T.ct[:, LT:LT + 6], [y1 - y0 for y0, y1 in zip(*ycol)], [3, 2])
     hcy = iota(T.ct[:, LY[1]:LY[1] + 3], [m + 4 * b2 for m in range(3)], [3])
+    iota(T.ct[:, CP:CP + 12], [(64 + 8 * t + 2 * c) if b2 else (16 * c + t) for t in range(3) for c in range(4)], [3, 4])
+    hcp = iota(T.ct[:, CP + 12:CP + 24], [t if b2 else (64 + 8 * t) for t in range(3) for c in range(4)], [3, 4])
+    hv32 = select(T.v32[:], T.ones[:, 0:32], [[-8, 2], [1, 4], [-1, 4]], A.is_equal, 8, 0, [])
 
     for b in range(4):
         hqe = quant("e", 128 * b, 128, T.et[:, 3 - b:515 - b], [he])
-    hz = quant("l0", 96, 128, T.dg[:, 304:816], [hdg])
+    ho = quant("l0", 96, 144, T.xo[:, 512:1088], [hown])
     h = mset(T.z[:, 0:8:2, ZQ:ZQ + 240:6], LOW)
     mset(T.z[:, 1:8:2, ZQ:ZQ + 240:5], LOW)
-    mset(T.cs[:, 1:8:2, CQ + 3:CQ + 84:3], 8.0)
-    fill(16)
-    mset(T.z[:, 0, ZQ + 6:ZQ + 7], 0.0, [h])
-    cp(T.cd[:, 1:8:2, 1:21:3], T.wj[:, 1:8:2, 1:8], [hwj])
-    cp(T.cd[:, 2:8:2, 1:28:4], T.wj[:, 2:8:2, 1:8], [hwj])
     ts(T.m4[:, 0:4], T.i8[:, 0:4], pq, A.is_equal, deps=[hi8, hpf])
+    mset(T.cs[:, 1:8:2, CQ + 3:CQ + 84:3], 8.0)
+    mset(T.z[:, 0, ZQ + 6:ZQ + 7], 0.0, [h])
+    for f in [(T.cd[:, 2:8:2, 2:28:4], 0.0), (T.cs[:, 1:8, CQ:CQ + 1], FIRST), (T.cs[:, 0, CQ:CQ + 84:12], FIRST), (T.cs[:, 0, CQ + 8:CQ + 84:12], FIRST),
+              (T.cs[:, 0:8:2, CQ + 4:CQ + 84:12], 8.0), (T.mt[:, 704:1024], 0.0)]:
+        mset(*f)
 
     free = {"d": None, "y": None}
 
@@ -260,39 +256,82 @@ def rank_program(g, core, T, topo):
                 h = act(T[dst][:, 4 * at + b:4 * (at + n):4], T.ps[:, BD + 512 * b + a:BD + 512 * b + a + n], 0.5, deps=[hs[b]])
         free["d"] = h
         return h
+    decode_cp(decode_mm(("l0", 96, 128), [ho]), "d0", [(0, 128, 128 * (1 - b0))])
     for k in range(8):
         hut = act(T.ut[:, 64 * k:64 * k + 64], T.u64[:], 4.0, deps=[hu64])
-    decode_cp(decode_mm(("o", 0, 128), [hoc, hos]), "d0", [(0, 128, 128 * (1 - b0))])
     for L in range(3):
-        hw8 = act(T.wd[:, WO[L] + ncol[L]:WO[L] + ncol[L] + 8], T.pwn[:, 0:8], deps=[hpw])
-    rts = {}
+        act(T.wd[:, WO[L] + ncol[L]:WO[L] + ncol[L] + 8], T.pwn[:, 0:8], deps=[hpw])
+    for k in range(4):
+        hw8 = act(T.wd[:, WO[2] + 4 * k:WO[2] + 4 * k + 4], T.pwn[:, 4 * (k // 2):4 * (k // 2) + 4])
+    w2 = T.wd[:, WO[2]:WO[2] + 16]
+    h = select(w2, w2, [[0, 2], [-2, 2], [0, 4]], A.is_ge, -64, 1, [hw8])
+    hwd.append(select(w2, w2, [[0, 2], [2, 2], [0, 4]], A.is_ge, 65, -1, [h]))
+    rts, H = {}, {}
 
-    def tables(L):
-        gams = [4 * (p["src"][1] - p["src"][0]) for p in pcs[L]]
-        for gam in gams:
+    def steps(L):
+        for p in pcs[L]:
+            gam = 4 * (p["src"][1] - p["src"][0])
             if gam not in rts:
                 k = 1 + len(rts)
                 rts[gam] = (T.rt[:, k:k + 1], ts(T.rt[:, k:k + 1], p4, float(gam), A.mult, pq, A.add, deps=[hpf]))
-        c = LA[L]
-        for p, gam in zip(pcs[L], gams):
-            m = len(p["key"]) // 4
-            hla = ts(T.ls[:, c:c + m], T.ct[:, c:c + m], rts[gam][0], A.add, deps=[rts[gam][1], hterm[L]])
-            c += m
-        return hla
-    tab = [tables(0), None, None]
-    hqu = quant("u", 0, 128, T.ut[:], [hut])
 
-    def level(L, lo, hi, prods, deps, dec, runs, dcols, mid=None):
+    def tables(L):
+        c = LA[L]
+        for p in pcs[L]:
+            m, (col, h) = len(p["key"]) // 4, rts[4 * (p["src"][1] - p["src"][0])]
+            H["la", L] = ts(T.ls[:, c:c + m], T.ct[:, c:c + m], col, A.add, deps=[h, hterm[L]])
+            c += m
+
+    def f_cd():
+        cp(T.cd[:, 1:8:2, 1:21:3], T.wj[:, 1:8:2, 1:8], [hwj])
+        cp(T.cd[:, 2:8:2, 1:28:4], T.wj[:, 2:8:2, 1:8], [hwj])
+
+    def f_u():
+        H["u"] = quant("u", 0, 128, T.ut[:], [hut])
+
+    def f_parts():
+        part(2, 0, 7)
+        part(3, 3, 1)
+        part(4, 0, 127)
+
+    def f_odd():
+        H["pj"] = part(5, 0, 1)
+
+    def f_pf():
+        H["pf"] = cp(T.pf[:, 2:6], T.pj[:, 2:6], [H["pj"]])
+        mset(T.mt[:, 1280:1536], 0.0)
+
+    def f_m4():
+        H["p8"] = ts(T.rt[:, 12:13], p8, 8.0, A.mult, deps=[H["pf"]])
+        H["y0"] = ts(T.rt[:, 13:14], ph, 7.0 if b1 else -7.0, A.mult, 1.0 if b1 else 8.0, A.add, deps=[H["pf"]])
+        for a, c in [(0, -1), (1, 36), (2, 67)]:
+            ts(T.m4[32 * a:32 * a + 32, 4:8], T.i8[32 * a:32 * a + 32, 0:4], float(c), A.add, T.pf[32 * a:32 * a + 32, 4:5], A.is_equal, deps=[H["pf"]])
+
+    def f_y():
+        H["y0"] = ts(T.rt[:, 11:12], T.rt[:, 13:14], p8, A.mult, deps=[H["y0"]])
+        H["y1"] = ts(T.rt[:, 14:15], ph, -4.0 if b2 else 4.0, A.mult, T.rt[:, 12:13], A.add, deps=[H["p8"]])
+
+    def f_y2():
+        H["y0"] = ts(T.ct[:, LT + 8:LT + 14], T.ct[:, LT:LT + 6], ph, A.mult, T.rt[:, 11:12], A.add, deps=[H["y0"], hcy])
+        ts(T.ls[:, LY[1]:LY[1] + 3], T.ct[:, LY[1]:LY[1] + 3], T.rt[:, 14:15], A.add, deps=[H["y1"], hcy])
+    spare = [lambda: steps(0), lambda: tables(0), f_cd, f_u, f_parts, f_odd, None, f_pf, f_m4, f_y, f_y2]
+
+    def gap():
+        if spare:
+            f = spare.pop(0)
+            if f is not None:
+                f()
+
+    def level(L, lo, hi, prods, deps, aside):
         n, v, up = ncol[L], WO[L], upper[L]
-        step = float(slots[L] if up else 1)
-        dw, am = T["d%d" % L][:, 0:4 * dcols], T["am%d" % L][:, 0:4 * n]
+        step = float(slots[L] if up and L < 2 else 1)
         for k, (st, mv) in enumerate(prods):
             hg = mm(BG, st, mv, k == 0, k == len(prods) - 1, deps)
-        hs = decode_mm(dec, deps)
         nt = 32 // slots[L]
         ht = {}
         for k in list(range(0, nt, 2)) + list(range(1, nt, 2)):
             ht[k % 2] = op("v", [hg], lambda: V.transpose(T.tt[lo:hi, k:8:nt, :], T.ps[lo:hi, BG + 32 // nt * k:BG + 32 // nt * k + 256 // nt]))
+        gap()
 
         def mask(f, par, s):
             c, k = 4 * (L % 2) + s, ZK[par]
@@ -303,16 +342,16 @@ def rank_program(g, core, T, topo):
             m = T.m4[lo:hi, c:c + 1]
             return act(o, i, m, deps=[d]) if f == "s" else ts(o, i, m, A.mult, deps=[d])
         ready = [[mask("s", 0, s) for s in (2, 3)] + [mask("v", 0, s) for s in (0, 1)], [mask("s", 1, s) for s in (2, 3)]]
-        hd = decode_cp(hs, "d%d" % L, runs)
-        ham = gat(am, dw.indirect(T.ls[:, LA[L]:LA[L] + n // 4]), [hd, tab[L]])
-        if mid is not None:
-            mid()
         z, cs, cd = T.z, T.cs, T.cd
         done = {}
         for tok in ORDER:
             k, j = tok[0], int(tok[1:])
             par = j % 2
-            if k == "e":
+            if k == "f":
+                gap()
+            elif k == "d":
+                aside()
+            elif k == "e":
                 ready[1].append(mask("v", 1, j))
             elif k in "sS":
                 o, st = ZO[par][k == "S"], 30 // ZK[par]
@@ -331,83 +370,149 @@ def rank_program(g, core, T, topo):
                     done[k, j] = tt(cd[lo:hi, j, c - 1:7 * c:c], z[lo:hi, j, was + 30:was + 240:30], z[lo:hi, j + 1, ZA + 30:ZA + 240:30], A.is_gt, deps=[done["s", j]])
         last = CO[1][0] + 80
         cuts = [(0, n + 8)] if n < 64 else [(0, n // 2), (n // 2, n + 8)]
+        gap()
         h = [ts(T.fa[lo:hi, a:b], T.wd[lo:hi, v + a:v + b], cs[lo:hi, 7, last:last + 1], A.mult, -0.5, A.add, deps=[done["k", 7], hwd[L], hw8]) for a, b in cuts]
+        gap()
         h = [ts(T.fb[lo:hi, a:b], T.fa[lo:hi, a:b], 7, A.bitwise_and, deps=[d]) for (a, b), d in zip(cuts, h)]
+        gap()
         hdig = [ts(T.dg[lo:hi, v + a:v + b], T.fb[lo:hi, a:b], step, A.mult, deps=[d]) for (a, b), d in zip(cuts, h)][-1]
-        h = quant("d", 0, 128, T.dg[:, v:v + 512], [hdig, hb])
-        hpt = act(T.ptf[lo:hi, 8 * L:8 * L + 8], T.dg[lo:hi, v + n:v + n + 8], 1.0 / step, deps=[hdig])
-        h = mm(BR, ("u", 0), ("d", 0, 128), True, True, [h, hqu])
-        o = T.off[:, OO[L]:OO[L] + n // 4]
-        h = ts(o, T.ps[:, BR:BR + n // 4], pq, A.add, deps=[h])
-        h = tt(T.mt[:, MO[L]:MO[L] + 4 * n], dw.indirect(o), am, A.add, deps=[h, ham])
-        return quant("m%d" % L, 0, 128, T.mt[:, MO[L]:MO[L] + 512], [h]), hpt
+        gap()
+        nd = 128 if L < 2 else 130
+        h = quant("d", 0, nd, T.dg[:, v:v + 4 * nd], [hdig, hb])
+        gap()
+        return h, act(T.ptf[lo:hi, 8 * L:8 * L + 8], T.dg[lo:hi, v + n:v + n + 8], 1.0 / step, deps=[hdig])
 
-    def outputs(L, hm, hqw, hly, at, n):
-        hy = [mm(BY + 512 * o, ("w", 128 * o), ("m%d" % L, 0, 128), True, True, [hm, hqw, free["y"]]) for o in range(2)]
-        hc = [act(T.yt[:, 256 * L + 128 * o:256 * L + 128 * o + 128], T.ps[:, BY + 512 * o:BY + 512 * o + 128], deps=[hy[o]]) for o in range(2)]
+    def merge(L, prods, deps, dec, runs, dcols):
+        n = ncol[L]
+        dw, am = T["d%d" % L][:, 0:4 * dcols], T["am%d" % L][:, 0:4 * n]
+
+        def aside():
+            hd = decode_cp(decode_mm(dec, deps), "d%d" % L, runs)
+            H["am"] = gat(am, dw.indirect(T.ls[:, LA[L]:LA[L] + n // 4]), [hd, H["la", L]])
+        h, hpt = level(L, 0, 96, prods, deps, aside)
+        h = mm(BR, ("u", 0), ("d", 0, 128), True, True, [h, H["u"]])
+        hl = ts(T.off[:, OO[L]:OO[L] + n // 4], T.ps[:, BR:BR + n // 4], pq, A.add, deps=[h])
+        gap()
+
+        def blend(a, k, w0):
+            return tt(T.mt[:, w0:w0 + 4 * k], dw.indirect(T.off[:, OO[L] + a // 4:OO[L] + (a + k) // 4]), am[:, 4 * a:4 * (a + k)], A.add, deps=[hl, H["am"]])
+        return blend, hpt
+
+    def products(m, n, hm, dst, w0):
+        hy = [mm(BY + 512 * o, ("w", 128 * o), (m, 0, n), True, True, [hm, hqw, free["y"]]) for o in range(2)]
+        hc = [act(T[dst][:, w0 + n * o:w0 + n * o + n], T.ps[:, BY + 512 * o:BY + 512 * o + n], deps=[hy[o]]) for o in range(2)]
         free["y"] = hc[1]
+        return hc
+
+    def outputs(L, hm, width, at, n):
+        hc = products("m%d" % L, width, hm, "yt", 384 * L)
         for o in range(2):
-            w0, y0 = 256 * L + 128 * o, 168 * o + at
-            h = gat(T.yo[:, y0:y0 + n], T.yt[:, w0:w0 + 128].indirect(T.ls[:, LY[L]:LY[L] + n // 16]), [hc[o], hly])
+            w0, y0 = 384 * L + width * o, 168 * o + at
+            h = gat(T.yo[:, y0:y0 + n], T.yt[:, w0:w0 + width].indirect(T.ls[:, LY[L]:LY[L] + n // 16]), [hc[o], hly])
             dma("y", "o1", [h, ha2], T.y[:, y0:y0 + n], T.yo[:, y0:y0 + n])
 
-    hm0, hpt = level(0, 0, 96, [(("l0", 0), ("o", 0, 144))], [ha1, hz, hoc, hos], ("l0", 0, 128), [(0, 128, 128 * b0)], 256)
-
-    plan = [(2, 0, 64), (6, 24, 256), (4, 48, 0)]
     es = [e for e in topo.engines(core, T.cores[r ^ 2]) if all(e in topo.engines(core, T.cores[r ^ x]) for x in (4, 6))]
-    k4 = len(es) // 4
-    sets = [[es[0:k4], es[k4:2 * k4], es[2 * k4:4 * k4]], [es[2 * k4:3 * k4], es[3 * k4:4 * k4], es[0:2 * k4]]]
-    wait("g", [hm0])
-    for kind in range(2):
-        trs = []
-        for (x, a, at), e in zip(plan, sets[kind]):
-            rid, pid = topo.addr(T.cores[r ^ x], core)
-            if kind == 0:
-                src, dst = T.qm0[:, a:a + 64].bitcast(dt.uint8), T.ql1[:, at:at + 64].bitcast(dt.uint8)
-            else:
-                src, dst = T.sm0[:, a:a + 64], T.sl1[:, at:at + 64]
-            trs.append(RemoteDMATransfer(dst_ids=[DstId(rid=rid, pnc=pid)], dma_engine_mask=bits(e), remote_sem=T.sem.a2, src=src, dst=dst))
-        g.remote_dma_fused(trs, local_sem=T.sem.loc)
-    count["loc"] += 8 * k4
-    ha2 = ("a2", 8 * k4)
+
+    def post(plan, h):
+        wait("g", [h])
+        k = len(es) // len(plan)
+        for kind in range(2):
+            trs = []
+            for n, (x, a, at) in enumerate(plan):
+                rid, pid = topo.addr(T.cores[r ^ x], core)
+                if kind == 0:
+                    src, dst = T.qm0[:, a:a + 64].bitcast(dt.uint8), T.ql1[:, at:at + 64].bitcast(dt.uint8)
+                else:
+                    src, dst = T.sm0[:, a:a + 64], T.sl1[:, at:at + 64]
+                trs.append(RemoteDMATransfer(dst_ids=[DstId(rid=rid, pnc=pid)], dma_engine_mask=bits(es[k * n:k * n + k]), remote_sem=T.sem.a2, src=src, dst=dst))
+            g.remote_dma_fused(trs, local_sem=T.sem.loc)
+        count["loc"] += 2 * len(es)
+
+    blend, hpt = merge(0, [(("l0", 0), ("l0", 96, 144))], [ha1, ho], ("l0", 0, 128), [(0, 128, 128 * b0)], 256)
+    h = blend(0, 48, 512)
+    blend(48, 24, 1024)
+    post([(2, 0, 64), (6, 24, 256)], quant("m0", 0, 128, T.mt[:, 512:1024], [h]))
+    h = blend(72, 40, 1120)
+    gap()
+    hm0 = quant("m0", 128, 128, T.mt[:, 1024:1536], [h])
+    post([(4, 128, 0)], hm0)
+    ha2 = ("a2", 4 * len(es))
     for a in range(3):
         dma("y", "o1", [hpt, ha2], T.pt[0:1, 32 * a:32 * a + 32], T.ptf[36 * a:36 * a + 4, 0:8])
 
-    decode_cp(decode_mm(("m0", 0, 128), [hm0]), "d1", [(48, 64, 0)])
-    hqw = quant("w", 0, 256, T.wt[:], [hw])
-    quant("m0", 128, 128, T.dg[:, 304:816], [hdg])
+    decode_cp(decode_mm(("m0", 128, 128), [hm0]), "d1", [(0, 64, 0)])
     hz1 = quant("l1", 128, 128, T.dg[:, 304:816], [hdg])
-    hp8 = ts(T.rt[:, 12:13], p8, 8.0, A.mult, deps=[hpf])
-    h0 = ts(T.rt[:, 13:14], ph, 7.0 if b1 else -7.0, A.mult, 1.0 if b1 else 8.0, A.add, deps=[hpf])
-    mset(T.mt[:, 448:544], 0.0)
-    for a, c in [(0, -1), (1, 36), (2, 67)]:
-        ts(T.m4[32 * a:32 * a + 32, 4:8], T.i8[32 * a:32 * a + 32, 0:4], float(c), A.add, T.pf[32 * a:32 * a + 32, 5:6], A.is_equal, deps=[hi8, hpf])
-    h0 = ts(T.rt[:, 11:12], T.rt[:, 13:14], p8, A.mult, deps=[h0])
-    h1 = ts(T.rt[:, 14:15], ph, -4.0 if b2 else 4.0, A.mult, T.rt[:, 12:13], A.add, deps=[hp8])
-    tab[1] = tables(1)
-    h0 = ts(T.ct[:, LT + 8:LT + 14], T.ct[:, LT:LT + 6], ph, A.mult, T.rt[:, 11:12], A.add, deps=[h0, hcy])
-    tab[2] = tables(2)
-    h0 = tt(T.ct[:, LT + 16:LT + 22], T.ct[:, LT + 8:LT + 14], T.ct[:, LY[0]:LY[0] + 6], A.add, deps=[h0])
-    ts(T.ls[:, LY[1]:LY[1] + 3], T.ct[:, LY[1]:LY[1] + 3], T.rt[:, 14:15], A.add, deps=[h1, hcy])
-    hly = cp(T.ls[:, LY[0]:LY[0] + 6], T.ct[:, LT + 16:LT + 22], [h0])
-    outputs(0, hm0, hqw, hly, 0, 96)
+    h = tt(T.ct[:, LT + 16:LT + 22], T.ct[:, LT + 8:LT + 14], T.ct[:, LY[0]:LY[0] + 6], A.add, deps=[H["y0"]])
+    heven = ts(T.rt[:, 9:10], odd, -1.0, A.mult, 1.0, A.add)
+    steps(1)
+    hqw = quant("w", 0, 256, T.wt[:], [hw])
+    hly = cp(T.ls[:, LY[0]:LY[0] + 6], T.ct[:, LT + 16:LT + 22], [h])
+    hr = ts(T.rt[:, 10:11], ph, 1.0 if b2 else 8.0, A.mult)
+    ts(T.rt[:, 8:9], ph, 64.0, A.mult, T.rt[:, 12:13], A.add)
+    if 1 - b0 in upper:
+        for f in gfill(1 - b0):
+            mset(*f)
+    tables(1)
+    outputs(0, hm0, 192, 0, 96)
+    act(T.vt[:, 0:32], T.v32[:], T.rt[:, 9:10], deps=[hv32, heven])
+    hvt = act(T.vt[:, 32:64], T.v32[:], odd)
 
-    hm1, hpt = level(1, 0, 96, [(("l1", 56), ("m0", 48, 128)), (("l1", 184), ("l1", 0, 128))], [ha2, hz1, hm0], ("l1", 0, 280),
-                     [(256, 24, 176), (0, 112, 64)], 200)
+    def f_lists():
+        ts(T.ls[:, LP:LP + 12], T.ct[:, CP:CP + 12], T.rt[:, 10:11], A.add, deps=[hcp, hr])
+        ts(T.ls[:, LP + 12:LP + 24], T.ct[:, CP + 12:CP + 24], T.rt[:, 12:13] if b2 else p8, A.add)
+
+    def f_vt():
+        for k in range(1, 8):
+            act(T.vt[:, 64 * k:64 * k + 64], T.vt[:, 0:64], deps=[hvt])
+        H["vt"] = act(T.vt[:, 512:528], T.vt[:, 0:16])
+
+    def f_v():
+        H["v"] = quant("v", 0, 132, T.vt[:], [H["vt"]])
+    spare += [f_lists, lambda: mset(T.mt[:, 352:512], 0.0), None, f_vt, None, None, None, None, f_v]
+
+    blend, hpt = merge(1, [(("l1", 56), ("m0", 128, 128)), (("l1", 184), ("l1", 0, 128))], [ha2, hz1, hm0], ("l1", 0, 280),
+                       [(256, 24, 176), (0, 112, 64)], 200)
+    hm1 = quant("m1", 0, 128, T.mt[:, 0:512], [blend(0, 88, 0)])
     for lo in range(2):
         for m in range(3):
             k = (lo ^ b2) + 2 * m
             dma("y", "o1", [hpt], T.pt[0:1, 96 + 8 * k:104 + 8 * k], T.ptf[36 * lo + m:36 * lo + m + 1, 8:16])
 
-    hm2, hpt = level(2, 64, 96, [(("m1", 0), ("m1", 0, 128))], [hm1], ("m1", 0, 128), [(0, 88, 0)], 88,
-                     lambda: outputs(1, hm1, hqw, hly, 96, 48))
+    runs = [("a", 0, T.ls[:, LP:LP + 12]), ("b", 0, T.ls[:, LP + 12:LP + 18]), ("b", 96, T.ls[:, LP + 18:LP + 24])]
+    got = [scales(d, a, "m1", 128, o, [hm1]) for d, a, o in runs]
+
+    def f_pick(k):
+        got.append(codes(runs[k][0], runs[k][1], "m1", 128, runs[k][2], [hm1]))
+
+    def aside():
+        outputs(1, hm1, 128, 96, 48)
+        hs = []
+        for b in range(4):
+            mm(BD + 512 * b, ("e", 128 * b), ("a", 0, 192), True, False, [free["d"]] + got)
+            hs.append(mm(BD + 512 * b, ("e", 128 * b), ("b", 0, 192), False, True, []))
+        H["pairs"] = decode_cp(hs, "pairs", [(0, 192, 0)])
+
+    def f_pairs():
+        H["c"] = quant("c", 0, 192, T.pairs[:], [H["pairs"]])
+        H["yp"] = products("c", 192, H["c"], "yp", 0)
+    f_pick(0)
+    spare += [lambda: f_pick(1), lambda: f_pick(2), None, f_pairs]
+    h, hpt = level(2, 64, 96, [(("m1", 0), ("m1", 0, 128))], [hm1], aside)
     dma("y", "o1", [hpt], T.pt[0:1, 144:168], T.ptf[64:67, 16:24])
-    hy = [mm(BY + 512 * o, ("w", 128 * o), ("m2", 0, 128), True, True, [hm2, free["y"]]) for o in range(2)]
-    dma("y", "o1", [hm2], T.oc[:, 0:96], T.qm2[:, 0:24].bitcast(dt.uint8))
-    for k in range(4):
-        dma("y" if k < 2 else "s", "o1" if k < 2 else "o2", [hm2], T.osc[4 * k:4 * k + 4, 0:24], T.sm2[32 * k:32 * k + 4, 0:24])
-    h = cp(T.yo[:, 144:168], T.ps[:, BY:BY + 24], [hy[0]])
-    dma("y", "o1", [h], T.y[:, 144:168], T.yo[:, 144:168])
-    h = act(T.yo[:, 312:336], T.ps[:, BY + 512:BY + 536], deps=[hy[1]])
-    dma("s", "o2", [h], T.y[:, 312:336], T.yo[:, 312:336])
+    mm(BR, ("v", 4), ("d", 0, 128), True, False, [h, H["v"]])
+    h = mm(BR, ("v", 0), ("d", 2, 128), False, True, [])
+    ts(T.off[:, 64:65], T.ps[:, BR:BR + 1], T.rt[:, 8:9], A.add, deps=[h])
+    h = ts(T.off[:, 65:66], T.ps[:, BR + 1:BR + 2], T.rt[:, 12:13], A.add, 128.0, A.add, deps=[h])
+    o = T.off[:, 64:66]
+    hs = scales("m2", 0, "c", 192, o, [h])
+    hy0 = cp(T.yz[:, 0:32], T.yp[:, 0:192].indirect(o), [h, H["yp"][0]])
+    hc = codes("m2", 0, "c", 192, o, [h])
+    hy1 = gat(T.yz[:, 32:64], T.yp[:, 192:384].indirect(o), [h, H["yp"][1]])
+    dma("y", "o1", [hy0], T.y[:, 144:168], T.yz[:, 0:24])
+    dma("y", "o1", [hc], T.oc[:, 0:96], T.qm2[:, 0:24].bitcast(dt.uint8))
+    dma("s", "o2", [hs], T.osc[8:12, 0:24], T.sm2[64:68, 0:24])
+    dma("s", "o2", [hy1], T.y[:, 312:336], T.yz[:, 32:56])
+    dma("s", "o2", [hs], T.osc[12:16, 0:24], T.sm2[96:100, 0:24])
+    for k in range(2):
+        dma("y", "o1", [hs], T.osc[4 * k:4 * k + 4, 0:24], T.sm2[32 * k:32 * k + 4, 0:24])
     wait("g", [(k, count[k]) for k in ("v", "s", "p", "g", "loc", "o1", "o2")])

from concourse.bass import DstId, RemoteDMATransfer
from concourse.mybir import dt, AluOpType, ActivationFunctionType

SCRATCH = {"ps": ("psum", [128, 4096], "float32")}
for _n, _w in dict(w=256, g=128, l0=240, l1=320, m0=256, m1=128, m2=32, e=512, u=128, v=132, d=132, a=192, b=192, c=192).items():
    SCRATCH["q" + _n] = ("sbuf", [128, _w], "float8_e4m3fn_x4")
    SCRATCH["s" + _n] = ("sbuf", [128, _w], "uint8")
for _d, _b in {"bfloat16": dict(xt=[24, 8, 4], xo=[1088], wt=[1024], et=[516], ut=[512], vt=[528], ones=[128], ident=[128], u64=[64], v32=[32],
                                dg=[816], mt=[1536], d0=[1024], d1=[800], am0=[448], am1=[352], pairs=[768]),
               "int32": dict(pi=[1], pj=[8], fa=[136], fb=[136]), "uint16": dict(ls=[128], off=[96]),
               "float32": dict(pf=[8], rt=[16], ct=[160], i8=[8], m4=[8], wd=[304], pwn=[48], pwb=[64], tt=[8, 32],
                               ge=[40, 4], go=[48, 4], he=[4, 40], ho=[4, 48],
                               z=[9, 272], cs=[8, 96], cd=[8, 28], wj=[8, 8], ptf=[24], yt=[640], yo=[336], yp=[384], yz=[64])}.items():
    for _n, _w in _b.items():
        SCRATCH[_n] = ("sbuf", [128] + _w, _d)
SEMAPHORES = ["v", "s", "p", "g", "ldx", "ldw", "a1", "a2", "loc", "o1", "o2"]
A = AluOpType
COPY = ActivationFunctionType.Copy
LOW = -1e29
FIRST = -2.0 ** -22
BG, BR, BY, BD = 0, 512, 1024, 2048
ZQ, ZK, ZO, ZP, ZA = 20, [5, 6], [(6, 31), (1, 25)], [30, 26], 6
CQ, CK, CO = 4, [4, 3], [(3, 7), (5, 8)]
ORDER = ("e1 e0 s0 S0 f0 s1 S1 f0 d0 a1 s2 S2 b1 b2 s3 S3 K1 k1 a2 b3 s4 S4 a3 K2 k2 a4 s5 S5 b4 k3 K3 b5 s6 S6 a5 K4 k4 b6 s7 a6 k5 K5 "
         "a7 b7 K6 k6 f0 k7").split()


def fit(vals, dims):
    steps, stride = [], len(vals)
    for n in dims:
        stride //= n
        steps.append(vals[stride] - vals[0] if n > 1 else 0)
    for k in range(len(vals)):
        rest, tot = k, vals[0]
        for n, st in zip(reversed(dims), reversed(steps)):
            tot += (rest % n) * st
            rest //= n
        assert tot == vals[k]
    return [[st, n] for st, n in zip(steps, dims)], vals[0]


def piece(kind, dims, f, high=0):
    idx = [[]]
    for n in dims:
        idx = [a + [k] for a in idx for k in range(n)]
    rows = [f(*a) for a in idx]
    return {"kind": kind, "dims": dims, "key": [t[0] for t in rows], "base": [t[1] - high for t in rows], "src": [t[2] for t in rows], "high": high}


def rank_program(g, core, T, topo):
    r = T.rank_of(core)
    if r is None:
        return
    b0, b1, b2 = r & 1, (r >> 1) & 1, (r >> 2) & 1
    V, S, P = g.vector, g.scalar, g.tensor
    queue = {"v": V, "s": S, "p": P, "g": g, "y": g.sync}
    count = {k: 0 for k in SEMAPHORES}
    seen = {}

    def wait(q, deps):
        need = {}
        for d in deps:
            if d is not None:
                need[d[0]] = max(need.get(d[0], 0), d[1])
        for s, n in need.items():
            if seen.get((q, s), 0) < n:
                queue[q].wait_ge(T.sem[s], n)
                seen[(q, s)] = n

    def op(q, deps, f):
        wait(q, deps)
        f().then_inc(T.sem[q], 1)
        count[q] += 1
        return (q, count[q])

    def dma(q, sem, deps, out, in_):
        wait(q, deps)
        queue[q].dma_start(out, in_).then_inc(T.sem[sem], 16)
        count[sem] += 16
        return (sem, count[sem])

    def iota(out, vals, dims, deps=()):
        pat, base = fit(vals, dims)
        return op("g", deps, lambda: g.iota(out, pat, base, 0, allow_small_or_imprecise_dtypes=True))

    def select(out, in_, pat, how, base, step, deps):
        return op("g", deps, lambda: g.affine_select(out, in_, pat, how, 0.0, base, step))

    def mset(ap, c, deps=()):
        return op("v", deps, lambda: V.memset(ap, c))

    def ts(out, in0, s1, o0, s2=None, o1=None, deps=()):
        if s2 is None:
            return op("v", deps, lambda: V.tensor_scalar(out, in0, s1, None, o0))
        return op("v", deps, lambda: V.tensor_scalar(out, in0, s1, s2, o0, o1))

    def tt(out, in0, in1, o, deps=()):
        return op("v", deps, lambda: V.tensor_tensor(out, in0, in1, o))

    def cp(out, in_, deps=()):
        return op("v", deps, lambda: V.tensor_copy(out, in_))

    def scan(out, d0, d1, first, o0, o1, deps):
        return op("v", deps, lambda: V.tensor_tensor_scan(out, d0, d1, first, o0, o1))

    def act(out, in_, scale=1.0, deps=()):
        return op("s", deps, lambda: S.activation(out, in_, COPY, scale=scale))

    def gat(out, in_, deps):
        return op("s", deps, lambda: S.activation(out, in_, COPY))

    def quant(n_, a, n, src, deps):
        return op("v", deps, lambda: V.quantize_mx(T["q" + n_][:, a:a + n], T["s" + n_][:, a:a + n], src))

    def mm(bank, st, mv, start, stop, deps):
        (s, sa), (m, ma, n) = st, mv
        return op("p", deps, lambda: P.matmul_mx(T.ps[:, bank:bank + n], T["q" + s][:, sa:sa + 128], T["s" + s][:, sa:sa + 128],
                                                 T["q" + m][:, ma:ma + n], T["s" + m][:, ma:ma + n], start, stop))

    def codes(dst, a, src, width, o, deps):
        n = 16 * o.shape[1]
        return cp(T["q" + dst][:, a:a + n].bitcast(dt.uint32), T["q" + src][:, 0:width].bitcast(dt.uint32).indirect(o), deps)

    def scales(dst, a, src, width, o, deps):
        return gat(T["s" + dst][:, a:a + 16 * o.shape[1]], T["s" + src][:, 0:width].indirect(o), deps)

    upper, slots = [b0, b1, b2], [16, 8, 8]

    def pair(L, key, blk, nat, i):
        return (key, blk, nat + i) if upper[L] else (key, nat, blk + slots[L] * i)

    def at0(x, lo, a, i):
        u = (x ^ b1) + 2 * (lo ^ b2)
        return pair(0, 36 * a + u, 128 * (1 - b0) + 4 * a + u, 128 * b0 + 32 * a + 8 * u, i)
    pcs = [[piece("nat", [2, 3, 8], lambda lo, a, i: at0(1, lo, a, i)), piece("blk", [8, 2, 4], lambda i, lo, a: at0(0, lo, a, i))],
           [piece("blk", [8, 2, 4], lambda i, lo, m: pair(1, 36 * lo + m, 4 * lo + m, 128 + 24 * lo + 8 * m, i), 0 if b1 else 128),
            piece("nat", [3, 8], lambda m, i: pair(1, 68 + m, 68 + m, 176 + 8 * m, i), 64 if b1 else 176)]]
    ncol = [sum(len(p["key"]) for p in pc) for pc in pcs] + [16]
    WO = [0, 144, 272]
    LA, LY, LP, LT, CP = [18, 50], [84, 90], 96, 96, 128
    OO = [0, 32, 64]

    def terms(L, deps):
        c = LA[L]
        for p in pcs[L]:
            n = len(p["key"])
            hk = iota(T.ct[:, c:c + n // 4], [4 * s for s in p["src"][0::4]], p["dims"][:-1] + ([2] if p["dims"][-1] == 8 else []), deps=deps)
            c += n // 4
        return hk

    def weights(L, deps):
        v = WO[L]
        for p in pcs[L]:
            n = len(p["key"])
            pat, base = fit(p["key"], p["dims"])
            hk = select(T.wd[:, v:v + n], T.pwb[:, 0:n] if p["kind"] == "blk" else T.pwn[:, 0:n], pat, A.is_equal, base, -1, deps)
            v += n
        return hk

    def bases(L, deps):
        v = WO[L]
        for p in pcs[L]:
            hk = iota(T.dg[96:97, v:v + len(p["key"])], p["base"], p["dims"], deps=deps)
            v += len(p["key"])
        return hk

    def gfill(up):
        if up:
            return [(T.he[:, :, 0:40:5], 0.0), (T.ho[:, :, 0:48:6], 0.0), (T.ho[:, :, 1:48:6], 0.0)]
        return [(T.ge[:, 0:40:5, :], 0.0), (T.go[:, 0:48:6, :], 0.0), (T.go[:, 1:48:6, :], 0.0)]

    hx = dma("y", "ldx", [], T.xt[:], T.x[:])
    hones = mset(T.ones[:], 1.0)
    hp = op("g", [], lambda: g.iota(T.pi[:], [[0, 1]], 0, 1))
    hi8 = iota(T.i8[:], list(range(8)), [8])
    hid = select(T.ident[:], T.ones[:], [[-1, 128]], A.is_equal, 0, 1, [hones])
    hu64 = select(T.u64[:], T.ones[:, 0:64], [[1, 4], [0, 4], [-1, 4]], A.is_equal, 0, 0, [])
    hterm = [terms(0, [])]
    hxo = mset(T.xo[:, 384:1088], 0.0)
    hdg = mset(T.dg[:], 0.0)

    def part(k, sh, mk):
        return ts(T.pj[:, k:k + 1], T.pi[:], sh, A.logical_shift_right, mk, A.bitwise_and, deps=[hp])
    part(0, 2, 3)
    hj = part(1, 0, 3)
    p4, pq, p8, ph, pp, odd = [T.pf[:, k:k + 1] for k in range(6)]
    for f in gfill(b0):
        mset(*f)

    for i in range(8):
        hpw = act(T.pwn[:, i:48:8], T.ones[:, 0:6], -8.0 ** (8 - i) if i else 0.0, deps=[hones])
    for e in range(4):
        act(T.et[:, e:512:4], T.ident[:], 1.0 if e == 3 else 0.0, deps=[hid])
    he = act(T.et[:, 512:516], T.ones[:, 0:4], 0.0)
    for i in range(8):
        hown = act(T.xo[:, 512 + 64 * i:560 + 64 * i], T.xt[:, b0:24:2, i, :], deps=[hx, hxo])
    for i in range(8):
        hpb = act(T.pwb[:, 8 * i:8 * i + 8], T.ones[:, 0:8], -8.0 ** (8 - i) if i else 0.0)
    for i in range(1, 8):
        hwj = act(T.wj[:, :, i], T.i8[:], -8.0 ** (i - 8), deps=[hi8])

    h = cp(T.xo[:, 0:384], T.xt[:, 1 - b0:24:2, :, :], [hx])
    hpf = cp(T.pf[:, 0:2], T.pj[:, 0:2], [hj])
    v, hh = WO[1], hdg
    for p in pcs[1]:
        if p["high"]:
            hh = mset(T.dg[96:98, v:v + len(p["key"])], float(p["high"]), [hdg])
        v += len(p["key"])
    hg0 = quant("g", 0, 128, T.xo[:, 0:512], [h, hxo])

    def bits(es):
        return sum(1 << e for e in es)
    mate = T.cores[r ^ 1]
    rid, pid = topo.addr(mate, core)
    es = topo.engines(core, mate)
    wait("g", [hg0])
    g.remote_dma(T.ql0[:, 0:96].bitcast(dt.uint8), T.qg[:, 0:96].bitcast(dt.uint8), T.sem.a1, T.sem.loc, pid, rid, bits(es))
    g.remote_dma(T.sl0[:, 0:96], T.sg[:, 0:96], T.sem.a1, T.sem.loc, pid, rid, bits(es))
    count["loc"] += 2 * len(es)
    ha1 = ("a1", 2 * len(topo.engines(mate, core)))
    hw = dma("y", "ldw", [ha1], T.wt[:], T.w[:])

    hwd = [weights(0, [hpw, hpb])]
    bases(0, [hh, hwd[0]])
    hb = bases(1, [])
    hterm.append(terms(1, [hb]))
    hwd.append(weights(1, []))
    ycol = [[(24 * (c ^ b2) + 8 * a) if k ^ b1 else (128 + 4 * (c ^ b2) + a) for a in range(3) for c in range(2)] for k in range(2)]
    iota(T.ct[:, LY[0]:LY[0] + 6], ycol[0], [3, 2])
    iota(T.ct[:, LT:LT + 6], [y1 - y0 for y0, y1 in zip(*ycol)], [3, 2])
    hcy = iota(T.ct[:, LY[1]:LY[1] + 3], [m + 4 * b2 for m in range(3)], [3])
    iota(T.ct[:, CP:CP + 12], [(64 + 8 * t + 2 * c) if b2 else (16 * c + t) for t in range(3) for c in range(4)], [3, 4])
    hcp = iota(T.ct[:, CP + 12:CP + 24], [t if b2 else (64 + 8 * t) for t in range(3) for c in range(4)], [3, 4])
    hv32 = select(T.v32[:], T.ones[:, 0:32], [[-8, 2], [1, 4], [-1, 4]], A.is_equal, 8, 0, [])

    for b in range(4):
        hqe = quant("e", 128 * b, 128, T.et[:, 3 - b:515 - b], [he])
    ho = quant("l0", 96, 144, T.xo[:, 512:1088], [hown])
    h = mset(T.z[:, 0:8:2, ZQ:ZQ + 240:6], LOW)
    mset(T.z[:, 1:8:2, ZQ:ZQ + 240:5], LOW)
    ts(T.m4[:, 0:4], T.i8[:, 0:4], pq, A.is_equal, deps=[hi8, hpf])
    mset(T.cs[:, 1:8:2, CQ + 3:CQ + 84:3], 8.0)
    mset(T.z[:, 0, ZQ + 6:ZQ + 7], 0.0, [h])
    for f in [(T.cd[:, 2:8:2, 2:28:4], 0.0), (T.cs[:, 1:8, CQ:CQ + 1], FIRST), (T.cs[:, 0, CQ:CQ + 84:12], FIRST), (T.cs[:, 0, CQ + 8:CQ + 84:12], FIRST),
              (T.cs[:, 0:8:2, CQ + 4:CQ + 84:12], 8.0), (T.mt[:, 704:1024], 0.0)]:
        mset(*f)

    free = {"d": None, "y": None}

    def decode_mm(mv, deps):
        return [mm(BD + 512 * b, ("e", 128 * b), mv, True, True, [hqe, free["d"]] + deps) for b in range(4)]

    def decode_cp(hs, dst, runs):
        for b in range(4):
            for (a, n, at) in runs:
                h = act(T[dst][:, 4 * at + b:4 * (at + n):4], T.ps[:, BD + 512 * b + a:BD + 512 * b + a + n], 0.5, deps=[hs[b]])
        free["d"] = h
        return h
    decode_cp(decode_mm(("l0", 96, 128), [ho]), "d0", [(0, 128, 128 * (1 - b0))])
    for k in range(8):
        hut = act(T.ut[:, 64 * k:64 * k + 64], T.u64[:], 4.0, deps=[hu64])
    for L in range(3):
        act(T.wd[:, WO[L] + ncol[L]:WO[L] + ncol[L] + 8], T.pwn[:, 0:8], deps=[hpw])
    for k in range(4):
        hw8 = act(T.wd[:, WO[2] + 4 * k:WO[2] + 4 * k + 4], T.pwn[:, 4 * (k // 2):4 * (k // 2) + 4])
    w2 = T.wd[:, WO[2]:WO[2] + 16]
    h = select(w2, w2, [[0, 2], [-2, 2], [0, 4]], A.is_ge, -64, 1, [hw8])
    hwd.append(select(w2, w2, [[0, 2], [2, 2], [0, 4]], A.is_ge, 65, -1, [h]))
    rts, H = {}, {}

    def steps(L):
        for p in pcs[L]:
            gam = 4 * (p["src"][1] - p["src"][0])
            if gam not in rts:
                k = 1 + len(rts)
                rts[gam] = (T.rt[:, k:k + 1], ts(T.rt[:, k:k + 1], p4, float(gam), A.mult, pq, A.add, deps=[hpf]))

    def tables(L):
        c = LA[L]
        for p in pcs[L]:
            m, (col, h) = len(p["key"]) // 4, rts[4 * (p["src"][1] - p["src"][0])]
            H["la", L] = ts(T.ls[:, c:c + m], T.ct[:, c:c + m], col, A.add, deps=[h, hterm[L]])
            c += m

    def f_cd():
        cp(T.cd[:, 1:8:2, 1:21:3], T.wj[:, 1:8:2, 1:8], [hwj])
        cp(T.cd[:, 2:8:2, 1:28:4], T.wj[:, 2:8:2, 1:8], [hwj])

    def f_u():
        H["u"] = quant("u", 0, 128, T.ut[:], [hut])

    def f_parts():
        part(2, 0, 7)
        part(3, 3, 1)
        part(4, 0, 127)

    def f_odd():
        H["pj"] = part(5, 0, 1)

    def f_pf():
        H["pf"] = cp(T.pf[:, 2:6], T.pj[:, 2:6], [H["pj"]])
        mset(T.mt[:, 1280:1536], 0.0)

    def f_m4():
        H["p8"] = ts(T.rt[:, 12:13], p8, 8.0, A.mult, deps=[H["pf"]])
        H["y0"] = ts(T.rt[:, 13:14], ph, 7.0 if b1 else -7.0, A.mult, 1.0 if b1 else 8.0, A.add, deps=[H["pf"]])
        for a, c in [(0, -1), (1, 36), (2, 67)]:
            ts(T.m4[32 * a:32 * a + 32, 4:8], T.i8[32 * a:32 * a + 32, 0:4], float(c), A.add, T.pf[32 * a:32 * a + 32, 4:5], A.is_equal, deps=[H["pf"]])

    def f_y():
        H["y0"] = ts(T.rt[:, 11:12], T.rt[:, 13:14], p8, A.mult, deps=[H["y0"]])
        H["y1"] = ts(T.rt[:, 14:15], ph, -4.0 if b2 else 4.0, A.mult, T.rt[:, 12:13], A.add, deps=[H["p8"]])

    def f_y2():
        H["y0"] = ts(T.ct[:, LT + 8:LT + 14], T.ct[:, LT:LT + 6], ph, A.mult, T.rt[:, 11:12], A.add, deps=[H["y0"], hcy])
        ts(T.ls[:, LY[1]:LY[1] + 3], T.ct[:, LY[1]:LY[1] + 3], T.rt[:, 14:15], A.add, deps=[H["y1"], hcy])
    spare = [lambda: steps(0), lambda: tables(0), f_cd, f_u, f_parts, f_odd, None, f_pf, f_m4, f_y, f_y2]

    def gap():
        if spare:
            f = spare.pop(0)
            if f is not None:
                f()

    def level(L, lo, hi, prods, deps, aside):
        n, v, up = ncol[L], WO[L], upper[L]
        step = float(slots[L] if up and L < 2 else 1)
        for k, (st, mv) in enumerate(prods):
            hg = mm(BG, st, mv, k == 0, k == len(prods) - 1, deps)
        nt = 32 // slots[L]
        ht = {}
        for k in list(range(0, nt, 2)) + list(range(1, nt, 2)):
            ht[k % 2] = op("v", [hg], lambda: V.transpose(T.tt[lo:hi, k:8:nt, :], T.ps[lo:hi, BG + 32 // nt * k:BG + 32 // nt * k + 256 // nt]))
        gap()

        def mask(f, par, s):
            c, k = 4 * (L % 2) + s, ZK[par]
            if up:
                o, i, d = [T.he, T.ho][par][lo:hi, :, 1 + par + s:8 * k:k], T.tt[lo:hi, par:8:2, 8 * s:8 * s + 8], ht[par]
            else:
                o, i, d = [T.ge, T.go][par][lo:hi, 1 + par + s:8 * k:k, :], T.tt[lo:hi, :, 8 * s + par:8 * s + 8:2], ht[1]
            m = T.m4[lo:hi, c:c + 1]
            return act(o, i, m, deps=[d]) if f == "s" else ts(o, i, m, A.mult, deps=[d])
        ready = [[mask("s", 0, s) for s in (2, 3)] + [mask("v", 0, s) for s in (0, 1)], [mask("s", 1, s) for s in (2, 3)]]
        z, cs, cd = T.z, T.cs, T.cd
        done = {}
        for tok in ORDER:
            k, j = tok[0], int(tok[1:])
            par = j % 2
            if k == "f":
                gap()
            elif k == "d":
                aside()
            elif k == "e":
                ready[1].append(mask("v", 1, j))
            elif k in "sS":
                o, st = ZO[par][k == "S"], 30 // ZK[par]
                gs = [T.he, T.ho][par][lo:hi, j // 2, :] if up else [T.ge, T.go][par][lo:hi, :, j // 2]
                done[k, j] = scan(z[lo:hi, j + 1, o:o + 240:st], z[lo:hi, j, ZQ:ZQ + 240:st], gs, LOW, A.max, A.add,
                                  [done.get(("s", j - 1)), done.get(("S", j - 1))] + ready[par])
            elif k in "kK":
                o, st = CO[par][k == "K"], 12 // CK[par]
                done[k, j] = scan(cs[lo:hi, j, o:o + 84:st], cd[lo:hi, j, 0:7 * CK[par]], cs[lo:hi, j - 1, CQ:CQ + 84:st], FIRST, A.add, A.min,
                                  [done["a", j], done["b", j], done.get(("k", j - 1)), done.get(("K", j - 1))])
            else:
                c, was, now = CK[par], ZP[1 - par], ZP[par]
                if k == "a":
                    done[k, j] = tt(cd[lo:hi, j, 0:7 * c:c], z[lo:hi, j, was:was + 210:30], z[lo:hi, j + 1, now:now + 210:30], A.is_ge, deps=[done["s", j]])
                else:
                    done[k, j] = tt(cd[lo:hi, j, c - 1:7 * c:c], z[lo:hi, j, was + 30:was + 240:30], z[lo:hi, j + 1, ZA + 30:ZA + 240:30], A.is_gt, deps=[done["s", j]])
        last = CO[1][0] + 80
        cuts = [(0, n + 8)] if n < 64 else [(0, n // 2), (n // 2, n + 8)]
        gap()
        h = [ts(T.fa[lo:hi, a:b], T.wd[lo:hi, v + a:v + b], cs[lo:hi, 7, last:last + 1], A.mult, -0.5, A.add, deps=[done["k", 7], hwd[L], hw8]) for a, b in cuts]
        gap()
        h = [ts(T.fb[lo:hi, a:b], T.fa[lo:hi, a:b], 7, A.bitwise_and, deps=[d]) for (a, b), d in zip(cuts, h)]
        gap()
        hdig = [ts(T.dg[lo:hi, v + a:v + b], T.fb[lo:hi, a:b], step, A.mult, deps=[d]) for (a, b), d in zip(cuts, h)][-1]
        gap()
        nd = 128 if L < 2 else 130
        h = quant("d", 0, nd, T.dg[:, v:v + 4 * nd], [hdig, hb])
        gap()
        return h, act(T.ptf[lo:hi, 8 * L:8 * L + 8], T.dg[lo:hi, v + n:v + n + 8], 1.0 / step, deps=[hdig])

    def merge(L, prods, deps, dec, runs, dcols):
        n = ncol[L]
        dw, am = T["d%d" % L][:, 0:4 * dcols], T["am%d" % L][:, 0:4 * n]

        def aside():
            hd = decode_cp(decode_mm(dec, deps), "d%d" % L, runs)
            H["am"] = gat(am, dw.indirect(T.ls[:, LA[L]:LA[L] + n // 4]), [hd, H["la", L]])
        h, hpt = level(L, 0, 96, prods, deps, aside)
        h = mm(BR, ("u", 0), ("d", 0, 128), True, True, [h, H["u"]])
        hl = ts(T.off[:, OO[L]:OO[L] + n // 4], T.ps[:, BR:BR + n // 4], pq, A.add, deps=[h])
        gap()

        def blend(a, k, w0):
            return tt(T.mt[:, w0:w0 + 4 * k], dw.indirect(T.off[:, OO[L] + a // 4:OO[L] + (a + k) // 4]), am[:, 4 * a:4 * (a + k)], A.add, deps=[hl, H["am"]])
        return blend, hpt

    def products(m, n, hm, dst, w0):
        hy = [mm(BY + 512 * o, ("w", 128 * o), (m, 0, n), True, True, [hm, hqw, free["y"]]) for o in range(2)]
        hc = [act(T[dst][:, w0 + n * o:w0 + n * o + n], T.ps[:, BY + 512 * o:BY + 512 * o + n], deps=[hy[o]]) for o in range(2)]
        free["y"] = hc[1]
        return hc

    def outputs(L, hm, width, at, n):
        hc = products("m%d" % L, width, hm, "yt", 384 * L)
        for o in range(2):
            w0, y0 = 384 * L + width * o, 168 * o + at
            h = gat(T.yo[:, y0:y0 + n], T.yt[:, w0:w0 + width].indirect(T.ls[:, LY[L]:LY[L] + n // 16]), [hc[o], hly])
            dma("y", "o1", [h, ha2], T.y[:, y0:y0 + n], T.yo[:, y0:y0 + n])

    es = [e for e in topo.engines(core, T.cores[r ^ 2]) if all(e in topo.engines(core, T.cores[r ^ x]) for x in (4, 6))]

    def post(plan, h):
        wait("g", [h])
        k = len(es) // len(plan)
        for kind in range(2):
            trs = []
            for n, (x, a, at) in enumerate(plan):
                rid, pid = topo.addr(T.cores[r ^ x], core)
                if kind == 0:
                    src, dst = T.qm0[:, a:a + 64].bitcast(dt.uint8), T.ql1[:, at:at + 64].bitcast(dt.uint8)
                else:
                    src, dst = T.sm0[:, a:a + 64], T.sl1[:, at:at + 64]
                trs.append(RemoteDMATransfer(dst_ids=[DstId(rid=rid, pnc=pid)], dma_engine_mask=bits(es[k * n:k * n + k]), remote_sem=T.sem.a2, src=src, dst=dst))
            g.remote_dma_fused(trs, local_sem=T.sem.loc)
        count["loc"] += 2 * len(es)

    blend, hpt = merge(0, [(("l0", 0), ("l0", 96, 144))], [ha1, ho], ("l0", 0, 128), [(0, 128, 128 * b0)], 256)
    h = blend(0, 48, 512)
    blend(48, 24, 1024)
    post([(2, 0, 64), (6, 24, 256)], quant("m0", 0, 128, T.mt[:, 512:1024], [h]))
    h = blend(72, 40, 1120)
    gap()
    hm0 = quant("m0", 128, 128, T.mt[:, 1024:1536], [h])
    post([(4, 128, 0)], hm0)
    ha2 = ("a2", 4 * len(es))
    for a in range(3):
        dma("y", "o1", [hpt, ha2], T.pt[0:1, 32 * a:32 * a + 32], T.ptf[36 * a:36 * a + 4, 0:8])

    decode_cp(decode_mm(("m0", 128, 128), [hm0]), "d1", [(0, 64, 0)])
    hz1 = quant("l1", 128, 128, T.dg[:, 304:816], [hdg])
    h = tt(T.ct[:, LT + 16:LT + 22], T.ct[:, LT + 8:LT + 14], T.ct[:, LY[0]:LY[0] + 6], A.add, deps=[H["y0"]])
    heven = ts(T.rt[:, 9:10], odd, -1.0, A.mult, 1.0, A.add)
    steps(1)
    hqw = quant("w", 0, 256, T.wt[:], [hw])
    hly = cp(T.ls[:, LY[0]:LY[0] + 6], T.ct[:, LT + 16:LT + 22], [h])
    hr = ts(T.rt[:, 10:11], ph, 1.0 if b2 else 8.0, A.mult)
    ts(T.rt[:, 8:9], ph, 64.0, A.mult, T.rt[:, 12:13], A.add)
    if 1 - b0 in upper:
        for f in gfill(1 - b0):
            mset(*f)
    tables(1)
    outputs(0, hm0, 192, 0, 96)
    act(T.vt[:, 0:32], T.v32[:], T.rt[:, 9:10], deps=[hv32, heven])
    hvt = act(T.vt[:, 32:64], T.v32[:], odd)

    def f_lists():
        ts(T.ls[:, LP:LP + 12], T.ct[:, CP:CP + 12], T.rt[:, 10:11], A.add, deps=[hcp, hr])
        ts(T.ls[:, LP + 12:LP + 24], T.ct[:, CP + 12:CP + 24], T.rt[:, 12:13] if b2 else p8, A.add)

    def f_vt():
        for k in range(1, 8):
            act(T.vt[:, 64 * k:64 * k + 64], T.vt[:, 0:64], deps=[hvt])
        H["vt"] = act(T.vt[:, 512:528], T.vt[:, 0:16])

    def f_v():
        H["v"] = quant("v", 0, 132, T.vt[:], [H["vt"]])
    spare += [f_lists, lambda: mset(T.mt[:, 352:512], 0.0), None, f_vt, None, None, None, None, f_v]

    blend, hpt = merge(1, [(("l1", 56), ("m0", 128, 128)), (("l1", 184), ("l1", 0, 128))], [ha2, hz1, hm0], ("l1", 0, 280),
                       [(256, 24, 176), (0, 112, 64)], 200)
    hm1 = quant("m1", 0, 128, T.mt[:, 0:512], [blend(0, 88, 0)])
    for lo in range(2):
        for m in range(3):
            k = (lo ^ b2) + 2 * m
            dma("y", "o1", [hpt], T.pt[0:1, 96 + 8 * k:104 + 8 * k], T.ptf[36 * lo + m:36 * lo + m + 1, 8:16])

    runs = [("a", 0, T.ls[:, LP:LP + 12]), ("b", 0, T.ls[:, LP + 12:LP + 18]), ("b", 96, T.ls[:, LP + 18:LP + 24])]
    got = [scales(d, a, "m1", 128, o, [hm1]) for d, a, o in runs]

    def f_pick(k):
        got.append(codes(runs[k][0], runs[k][1], "m1", 128, runs[k][2], [hm1]))

    def aside():
        outputs(1, hm1, 128, 96, 48)
        hs = []
        for b in range(4):
            mm(BD + 512 * b, ("e", 128 * b), ("a", 0, 192), True, False, [free["d"]] + got)
            hs.append(mm(BD + 512 * b, ("e", 128 * b), ("b", 0, 192), False, True, []))
        H["pairs"] = decode_cp(hs, "pairs", [(0, 192, 0)])

    def f_pairs():
        H["c"] = quant("c", 0, 192, T.pairs[:], [H["pairs"]])
        H["yp"] = products("c", 192, H["c"], "yp", 0)
    f_pick(0)
    spare += [lambda: f_pick(1), lambda: f_pick(2), None, f_pairs]
    h, hpt = level(2, 64, 96, [(("m1", 0), ("m1", 0, 128))], [hm1], aside)
    dma("y", "o1", [hpt], T.pt[0:1, 144:168], T.ptf[64:67, 16:24])
    mm(BR, ("v", 4), ("d", 0, 128), True, False, [h, H["v"]])
    h = mm(BR, ("v", 0), ("d", 2, 128), False, True, [])
    ts(T.off[:, 64:65], T.ps[:, BR:BR + 1], T.rt[:, 8:9], A.add, deps=[h])
    h = ts(T.off[:, 65:66], T.ps[:, BR + 1:BR + 2], T.rt[:, 12:13], A.add, 128.0, A.add, deps=[h])
    o = T.off[:, 64:66]
    hs = scales("m2", 0, "c", 192, o, [h])
    hy0 = cp(T.yz[:, 0:32], T.yp[:, 0:192].indirect(o), [h, H["yp"][0]])
    hc = codes("m2", 0, "c", 192, o, [h])
    hy1 = gat(T.yz[:, 32:64], T.yp[:, 192:384].indirect(o), [h, H["yp"][1]])
    dma("y", "o1", [hy0], T.y[:, 144:168], T.yz[:, 0:24])
    dma("y", "o1", [hc], T.oc[:, 0:96], T.qm2[:, 0:24].bitcast(dt.uint8))
    dma("s", "o2", [hs], T.osc[8:12, 0:24], T.sm2[64:68, 0:24])
    dma("s", "o2", [hy1], T.y[:, 312:336], T.yz[:, 32:56])
    dma("s", "o2", [hs], T.osc[12:16, 0:24], T.sm2[96:100, 0:24])
    for k in range(2):
        dma("y", "o1", [hs], T.osc[4 * k:4 * k + 4, 0:24], T.sm2[32 * k:32 * k + 4, 0:24])
    wait("g", [(k, count[k]) for k in ("v", "s", "p", "g", "loc", "o1", "o2")])
